import numpy as np, ml_dtypes
CORES = [16,18,20,22]
N = 4
BF = ml_dtypes.bfloat16
def gentries(a):
    return np.ascontiguousarray(a.reshape(8, 16, -1).transpose(0, 2, 1)).reshape(8, -1)
def gtable(e):
    e = np.asarray(e); return np.ascontiguousarray(e.reshape(8, -1, 16).transpose(0, 2, 1)).reshape(128, -1).astype(np.int32)
W, n, V, C, Z = 3, 4096, 8192, 2048, 1024
def counts(rng, h, z):
    c = np.zeros((N, 8, W), np.int64)
    for r in range(N):
        for g in range(8):
            m = int(h[r, g] - z[r, g]) - (W - 2); b = np.sort(rng.integers(0, m + 1, W - 3))
            c[r, g, 0] = n - h[r, g]; c[r, g, 1:W - 1] = np.diff(np.concatenate([[0], b, [m]])) + 1; c[r, g, W - 1] = z[r, g]
    return c
def some(rng):
    return rng.integers(C - C // 4, C + 1, (N, 8)), rng.integers(Z // 2, Z + 1, (N, 8))
def names(rng):
    return np.stack([np.stack([rng.permutation(V)[:n] for g in range(8)]) for r in range(N)]).astype(np.int64)
def depths(rng, c):
    return np.stack([np.stack([rng.permutation(np.repeat(np.arange(W), c[r, g])) for g in range(8)]) for r in range(N)])
def link(rng, o, dep):
    x = np.zeros((N, 8, n), np.int64)
    for r in range(N):
        q = (r + 1) % N
        for g in range(8):
            m = np.ones(V, bool); m[o[q, g]] = False; free = np.flatnonzero(m)
            v = free[rng.integers(0, len(free), n)]
            for k in range(1, W):
                i = np.flatnonzero(dep[r, g] == k)
                if len(i):
                    t = np.flatnonzero(dep[q, g] == k - 1 if k < W - 1 else dep[q, g] >= W - 2)
                    v[i] = o[q, g][t[rng.integers(0, len(t), len(i))]]
            x[r, g] = v
    return x
def pack(o, x, s):
    return {"own": np.stack([gtable(a) for a in o]), "nxt": np.stack([gtable(a) for a in x]), "pts": np.asarray(s).astype(np.int32)}
def points(rng):
    return rng.integers(0, 256, (N, 8, n))
def setup_inputs(rng):
    h, z = some(rng); o = names(rng); dep = depths(rng, counts(rng, h, z))
    return pack(o, link(rng, o, dep), points(rng))
def setup_inputs_full(rng):
    o = names(rng); c = counts(rng, np.full((N, 8), C), np.full((N, 8), Z)); e = rng.permutation(8)[:4]
    c[:, e, 1:W - 2] = 1; c[:, e, W - 2] = C - Z - (W - 3)
    dep = depths(rng, c)
    return pack(o, link(rng, o, dep), points(rng))
def setup_inputs_few(rng):
    h, z = some(rng); e = rng.permutation(8); q = int(rng.integers(0, N)); o = names(rng)
    z[:, e[2]] = 1; z[:, e[3]] = np.where(rng.random(N) < 0.5, 0, z[:, e[3]]); z[q, e[3]] = 0; z[:, e[4]] = Z; h[:, e[4]] = C
    c = counts(rng, h, z); c[:, e[0], 0] = n; c[:, e[0], 1:] = 0
    for t in range(W - 1):
        r = (q - t) % N; c[r, e[1], 0] += np.sum(c[r, e[1], t + 1:]); c[r, e[1], t + 1:] = 0
    dep = depths(rng, c)
    return pack(o, link(rng, o, dep), points(rng))
def setup_inputs_repeats(rng):
    h, z = some(rng); o = names(rng); dep = depths(rng, counts(rng, h, z)); x = link(rng, o, dep)
    for r in range(N):
        for g in range(8):
            for k in (0, W - 1):
                i = np.flatnonzero(dep[r, g] == k); x[r, g, i] = x[r, g, i[0]]
    return pack(o, x, points(rng))
def setup_inputs_ends(rng):
    h, z = some(rng); dep = depths(rng, counts(rng, h, z))
    o = 1 + np.stack([np.stack([rng.permutation(V - 2)[:n] for g in range(8)]) for r in range(N)]).astype(np.int64)
    for r in range(N):
        for g in range(0, 8, 2):
            o[r, g, 0] = 0; o[r, g, n - 1] = V - 1; a = dep[r, g]
            i = np.flatnonzero(a == W - 1); j = i[rng.integers(0, len(i))]; u, v = int(a[0]), int(a[j]); a[j] = u; a[0] = v
            i = np.flatnonzero(a[1:] == W - 1) + 1; j = i[rng.integers(0, len(i))]; u, v = int(a[n - 1]), int(a[j]); a[j] = u; a[n - 1] = v
    x = link(rng, o, dep)
    x[:, 0::2, 0] = V - 1; x[:, 0::2, n - 1] = 0
    for g in range(1, 8, 2):
        m = (dep[:, g] == 0) & (rng.random((N, n)) < 0.5)
        x[:, g] = np.where(m, rng.integers(0, 2, (N, n)) * (V - 1), x[:, g])
    return pack(o, x, 255 * rng.integers(0, 2, (N, 8, n)))
def setup_inputs_spread(rng):
    z = np.maximum(Z >> rng.integers(0, 7, (N, 8)), 1); h = z + np.maximum((C - Z) >> rng.integers(0, 7, (N, 8)), W - 2)
    o = np.stack([np.stack([(rng.integers(0, V) + rng.permutation(n + n // 8)[:n]) % V for g in range(8)]) for r in range(N)]).astype(np.int64)
    o[:, 1::2] = np.sort(o[:, 1::2], axis=2)
    dep = depths(rng, counts(rng, h, z))
    return pack(o, link(rng, o, dep), 255 >> rng.integers(0, 9, (N, 8, n)))
def followers(o, x):
    to = np.zeros((N, 8, n), np.int64)
    for r in range(N):
        for g in range(8):
            where = np.full(V, -1, np.int64); where[o[(r + 1) % N, g]] = np.arange(n); to[r, g] = where[x[r, g]]
    return to
def step(p, v, t):
    return np.take_along_axis(np.roll(v, -t, axis=0), p, axis=2)
def chains(to, s):
    p = np.broadcast_to(np.arange(n), (N, 8, n)); tot = s.astype(np.int64)
    for t in range(1, W):
        p = np.where(p >= 0, step(np.maximum(p, 0), to, t - 1), -1)
        tot = tot + np.where(p >= 0, step(np.maximum(p, 0), s, t), 0)
    return p, tot
def check_inputs(d):
    try:
        o = np.stack([gentries(a) for a in d["own"]]).astype(np.int64); x = np.stack([gentries(a) for a in d["nxt"]]).astype(np.int64); s = np.asarray(d["pts"]).astype(np.int64)
        if o.shape != (N, 8, n) or x.shape != (N, 8, n) or s.shape != (N, 8, n): return ["shapes"]
        bad = []
        if s.min() < 0 or s.max() > 255: bad.append("points")
        if o.min() < 0 or o.max() >= V or x.min() < 0 or x.max() >= V: return bad + ["names in range"]
        if (np.diff(np.sort(o, axis=2), axis=2) == 0).any(): return bad + ["own names differ"]
        to = followers(o, x); p, tot = chains(to, s)
        if np.max(np.count_nonzero(to >= 0, axis=2)) > C: bad.append("followers")
        if np.max(np.count_nonzero(p >= 0, axis=2)) > Z: bad.append("kept")
        return bad
    except Exception:
        return ["shapes"]
def reference(own, nxt, pts):
    o = np.stack([gentries(a) for a in own]).astype(np.int64); x = np.stack([gentries(a) for a in nxt]).astype(np.int64)
    p, tot = chains(followers(o, x), pts)
    yk = np.full((N, 8, Z), -1, np.float32); ys = np.zeros((N, 8, Z), np.float32)
    for r in range(N):
        for g in range(8):
            i = np.flatnonzero(p[r, g] >= 0)
            yk[r, g, :len(i)] = o[r, g, i]; ys[r, g, :len(i)] = tot[r, g, i]
    return {"yk": yk, "ys": ys}

@@ -1,0 +1,333 @@
+from concourse.mybir import AluOpType as A, ActivationFunctionType as F
+
+SCRATCH = {
+    "owi": ("sbuf", [128, 256], "int32"),
+    "pti": ("sbuf", [128, 256], "int32"),
+    "nxi": ("sbuf", [128, 256], "int32"),
+    "pf": ("sbuf", [128, 256], "float32"),
+    "pb": ("sbuf", [128, 256], "bfloat16"),
+    "own1": ("sbuf", [128, 256], "int32"),
+    "pf1": ("sbuf", [128, 256], "float32"),
+    "ol": ("sbuf", [128, 256], "uint16"),
+    "nl": ("sbuf", [128, 256], "uint16"),
+    "jl": ("sbuf", [128, 256], "uint16"),
+    "D": ("sbuf", [128, 4096], "float32"),
+    "WA": ("sbuf", [128, 8192], "bfloat16"),
+    "WB": ("sbuf", [128, 8192], "float32"),
+    "bg": ("sbuf", [128, 4096], "bfloat16"),
+    "R": ("sbuf", [128, 4096], "bfloat16"),
+    "V2": ("sbuf", [128, 4112], "bfloat16"),
+    "R2": ("sbuf", [128, 4096], "bfloat16"),
+    "prow": ("sbuf", [8, 4096], "bfloat16"),
+    "lt": ("sbuf", [128, 256], "float32"),
+    "ht": ("sbuf", [128, 256], "float32"),
+    "pid": ("sbuf", [128, 1], "int32"),
+    "pm": ("sbuf", [128, 1], "int32"),
+    "hcol": ("sbuf", [128, 1], "float32"),
+    "ccol": ("sbuf", [128, 1], "float32"),
+    "ci": ("sbuf", [128, 16], "float32"),
+    "cst": ("sbuf", [128, 16], "float32"),
+    "BI": ("sbuf", [128, 144], "bfloat16"),
+    "B2": ("sbuf", [128, 144], "bfloat16"),
+    "B0": ("sbuf", [128, 144], "bfloat16"),
+    "B8": ("sbuf", [128, 144], "bfloat16"),
+    "E": ("sbuf", [128, 144], "bfloat16"),
+    "E16": ("sbuf", [128, 144], "float16"),
+    "E4k": ("sbuf", [128, 144], "float16"),
+    "SG": ("sbuf", [128, 128], "bfloat16"),
+    "LS": ("sbuf", [128, 128], "bfloat16"),
+    "NL": ("sbuf", [128, 128], "bfloat16"),
+    "ones": ("sbuf", [128, 256], "float32"),
+    "d3": ("sbuf", [128, 256], "bfloat16"),
+    "mi": ("sbuf", [128, 1024], "float32"),
+    "mk": ("sbuf", [128, 2320], "bfloat16"),
+    "blk": ("sbuf", [128, 1024], "bfloat16"),
+    "bl": ("sbuf", [128, 64], "uint16"),
+    "o1": ("sbuf", [128, 256], "int32"),
+    "x1": ("sbuf", [128, 256], "int32"),
+    "par": ("sbuf", [128, 256], "int32"),
+    "parc": ("sbuf", [128, 256], "float32"),
+    "base0": ("sbuf", [128, 256], "float32"),
+    "base": ("sbuf", [128, 256], "float32"),
+    "kept": ("sbuf", [128, 256], "bfloat16"),
+    "zx": ("sbuf", [128, 32], "bfloat16"),
+    "e0": ("sbuf", [128, 16], "float32"),
+    "e1": ("sbuf", [128, 16], "float32"),
+    "p1": ("sbuf", [128, 16], "float32"),
+    "zl": ("sbuf", [128, 16], "uint16"),
+    "cum": ("sbuf", [128, 256], "float32"),
+    "KW": ("sbuf", [128, 256], "float32"),
+    "XW": ("sbuf", [128, 256], "float32"),
+    "YW": ("sbuf", [128, 256], "float32"),
+    "hit": ("sbuf", [128, 1024], "float16"),
+    "hx": ("sbuf", [128, 1024], "float16"),
+    "hy": ("sbuf", [128, 1024], "float16"),
+    "pa": ("sbuf", [128, 64], "float32"),
+    "pc": ("sbuf", [128, 64], "float32"),
+    "ok": ("sbuf", [128, 64], "float32"),
+    "osum": ("sbuf", [128, 64], "float32"),
+}
+for _k in range(8):
+    SCRATCH["b%d" % _k] = ("psum", [128, 512], "float32")
+SEMAPHORES = ["v", "a", "t", "p", "down", "dpts", "dnxt", "drow", "dpr", "dprow", "dout",
+              "rown", "rpts", "rv", "sent"]
+
+
+def rank_program(g, core, T, topo):
+    rank = T.rank_of(core)
+    if rank is None:
+        return
+    prev = T.cores[(rank - 1) % 4]
+    rid, pid, _se = topo.addr(prev)
+    eng = topo.engines(core, prev)
+    half = len(eng) // 2
+    maskA = sum(1 << e for e in eng[:half])
+    maskB = sum(1 << e for e in eng[half:])
+    mask = topo.mask(core, prev)
+    queues = {"v": g.vector, "a": g.scalar, "t": g.tensor, "p": g, "s": g.sync}
+    cnt = {}
+    seen = {}
+
+    def need(q, toks):
+        best = {}
+        for s, n in toks:
+            best[s] = max(best.get(s, 0), n)
+        for s in sorted(best):
+            if seen.get((q, s), 0) < best[s]:
+                queues[q].wait_ge(T.sem[s], best[s])
+                seen[(q, s)] = best[s]
+
+    def done(s, ins, n):
+        cnt[s] = cnt.get(s, 0) + n
+        ins.then_inc(T.sem[s], n)
+        return (s, cnt[s])
+
+    def V(toks, name, *args):
+        need("v", toks)
+        q = g.vector
+        if name == "ts":
+            out, in0, s1, s2, op0 = args[:5]
+            ins = q.tensor_scalar(out, in0, s1, s2, op0, args[5]) if len(args) > 5 else q.tensor_scalar(out, in0, s1, s2, op0)
+        elif name == "tt":
+            ins = q.tensor_tensor(*args)
+        elif name == "cp":
+            ins = q.tensor_copy(*args)
+        elif name == "ms":
+            ins = q.memset(*args)
+        else:
+            ins = q.tensor_tensor_scan(*args)
+        return done("v", ins, 1)
+
+    def ACT(toks, out, in_, func):
+        need("a", toks)
+        return done("a", g.scalar.activation(out, in_, func), 1)
+
+    def IOTA(toks, out, pattern, base, cm, small=True):
+        need("p", toks)
+        ins = g.iota(out, pattern, base, cm, allow_small_or_imprecise_dtypes=True) if small else g.iota(out, pattern, base, cm)
+        return done("p", ins, 1)
+
+    def SEL(toks, out, in_, pattern, cmp, fill, base, cm):
+        need("p", toks)
+        return done("p", g.affine_select(out, in_, pattern, cmp, fill, base, cm), 1)
+
+    def DMA(q, s, toks, out, in_):
+        need(q, toks)
+        return done(s, queues[q].dma_start(out, in_), 16)
+
+    def MM(toks, jobs, tok=True):
+        need("t", toks)
+        ins = None
+        for out, lhs, rhs, st, sp in jobs:
+            ins = g.tensor.matmul(out, lhs, rhs, st, sp)
+        return done("t", ins, 1) if tok else None
+
+    def SEND(toks, dst, src, sem, m):
+        need("p", toks)
+        g.remote_dma(out_ap=dst, in_ap=src, remote_sem=T.sem[sem], local_sem=T.sem.sent, pid=pid, routing_id=rid,
+                     dma_engine_mask=m)
+        n = bin(m).count("1")
+        cnt["sent"] = cnt.get("sent", 0) + n
+        cnt[sem] = cnt.get(sem, 0) + n
+
+    def rewrap(out, mat, src, c0, c1, K=128):
+        return [(out, mat[0:K, 15 - t:143 - t], src[0:K, 16 * c0 + t:16 * c1:16], t == 0, t == 15) for t in range(16)]
+
+    l_own = DMA("s", "down", [], T.owi[:], T.own[:])
+    l_pts = DMA("a", "dpts", [], T.pti[:], T.pts[:])
+    l_nxt = DMA("s", "dnxt", [], T.nxi[:], T.nxt[:])
+
+    c_pid = IOTA([], T.pid[:], [[1, 1]], 0, 1, False)
+    c_lt = IOTA([], T.lt[:], [[-16, 256]], 4096, 0)
+    z0 = V([], "ms", T.WB[:, 0:512], 0.0)
+    a1 = ACT([z0], T.WB[:, 512:1024], T.WB[:, 0:512], F.Silu)
+    a2 = ACT([a1], T.D[:, 3072:4096], T.WB[:, 0:1024], F.Silu)
+    a3 = ACT([a1], T.WB[:, 1024:2048], T.WB[:, 0:1024], F.Silu)
+    a4 = ACT([a3], T.WB[:, 2048:4096], T.WB[:, 0:2048], F.Silu)
+    a5 = ACT([a3], T.WB[:, 4096:6144], T.WB[:, 0:2048], F.Silu)
+    V([], "ms", T.D[:, 0:2048], 0.0)
+    v_pf = V([l_pts], "ts", T.pf[:], T.pti[:], 16.0, 16.0, A.mult, A.add)
+    v_pm = V([c_pid], "ts", T.pm[:], T.pid[:], 15, None, A.bitwise_and)
+    v_d = V([], "ms", T.D[:, 2048:3072], 0.0)
+    v_h = V([v_pm], "ts", T.hcol[:], T.pm[:], -16.0, 240.0, A.mult, A.add)
+    v_ht = V([v_h, c_lt], "ts", T.ht[:], T.lt[:], 0.0, T.hcol[:], A.mult, A.add)
+    SEND([l_own], T.own1[:], T.owi[:], "rown", maskA)
+    SEND([v_pf], T.pf1[:], T.pf[:], "rpts", maskB)
+    r_own = ("rown", half)
+    r_pts = ("rpts", half)
+    DMA("s", "drow", [v_d, a2, c_lt], T.D[1::16, :], T.lt[:])
+    d_lh = DMA("s", "drow", [v_ht], T.D[0::16, :], T.ht[:])
+    d_pr = DMA("s", "dpr", [r_pts], T.D[2::16, :], T.pf1[:])
+
+    p_z1 = IOTA([], T.WB[:, 6144:7168], [[0, 1024]], 0, 0)
+    p_z2 = IOTA([], T.WB[:, 7168:8192], [[0, 1024]], 0, 0)
+    v_wa = V([], "ms", T.WA[:], 0.0)
+    for b in ("BI", "B2", "B0", "B8"):
+        v_z = V([], "ms", T[b][:], 0.0)
+    V([], "ms", T.V2[:, 4096:4112], 0.0)
+    v_zx = V([], "ms", T.zx[:], 0.0)
+    v_nl = V([l_nxt], "cp", T.nl[:], T.nxi[:])
+    v_olb = V([r_own], "cp", T.ol[:, 128:256], T.own1[:, 128:256])
+    v_ola = V([], "cp", T.ol[:, 0:128], T.own1[:, 0:128])
+    v_pb = V([l_pts], "ts", T.pb[:], T.pti[:], 1.0, None, A.mult)
+
+    s_b = ACT([a5, p_z2, v_olb, d_lh, d_pr], T.WB[:].indirect(T.ol[:, 128:256]), T.D[:, 2048:4096], F.Silu)
+    s_a = V([v_wa, v_ola, d_lh, d_pr], "cp", T.WA[:].indirect(T.ol[:, 0:128]), T.D[:, 0:2048])
+    d_prow = DMA("s", "dprow", [v_pb], T.prow[:], T.pb[:])
+
+    def rowsel(buf, fills):
+        tok = v_z
+        for k, w in fills:
+            tok = SEL([tok], buf[:], buf[:], [[-16, 9], [0, 16]], A.not_equal, w, -k, 1)
+        return SEL([tok], buf[:], buf[:], [[0, 9], [1, 16]], A.is_equal, 0.0, -15, 0)
+
+    m_bi = rowsel(T.BI, [(0, 16.0), (1, 0.0625)])
+    m_b2 = rowsel(T.B2, [(2, 0.0625)])
+    m_b8 = SEL([v_z], T.B8[:], T.B8[:], [[-1, 144]], A.not_equal, 1.0, 15, 16)
+    c_d3 = IOTA([], T.d3[:], [[16, 16], [256, 16]], 0, 0)
+    c_ci = IOTA([], T.ci[:], [[1, 16]], 1025, 0)
+    c_mi = IOTA([], T.mi[:], [[1, 1024]], 0, 0)
+
+    t_pts = MM([m_b8, d_prow], rewrap(T.b7[:, 0:256], T.B8, T.prow, 0, 256, 8))
+
+    subs = [(k * 32, k * 32 + 32) for k in range(8)]
+    g_a = [ACT([s_b, v_nl], T.bg[:, 16 * c0:16 * c1], T.WB[:].indirect(T.nl[:, c0:c1]), F.Copy) for c0, c1 in subs]
+    g_v = [None] * 4
+    t_code = [None] * 4
+    t_fp = [None] * 4
+    v_jl = [None] * 4
+
+    def jl(q):
+        v_jl[q] = V([t_code[q]], "ts", T.jl[:, 64 * q:64 * q + 64], T["b%d" % q][:, 0:64], -1.0, 4096.0, A.mult, A.add)
+
+    def fp(q):
+        t_fp[q] = MM([g_v[q], m_b2], rewrap(T.b6[:, 64 * q:64 * q + 64], T.B2, T.R, 64 * q, 64 * q + 64))
+
+    for q in range(4):
+        for k in (2 * q, 2 * q + 1):
+            c0, c1 = subs[k]
+            g_v[q] = V([s_a, g_a[k], v_nl], "tt", T.R[:, 16 * c0:16 * c1], T.WA[:].indirect(T.nl[:, c0:c1]),
+                       T.bg[:, 16 * c0:16 * c1], A.add)
+        SEND([g_v[q]], T.V2[:, 1024 * q:1024 * q + 1024], T.R[:, 1024 * q:1024 * q + 1024], "rv", mask)
+        t_code[q] = MM([g_v[q], m_bi], rewrap(T["b%d" % q][:, 0:64], T.BI, T.R, 64 * q, 64 * q + 64))
+        if q >= 1:
+            fp(q - 1)
+        if q >= 2:
+            jl(q - 2)
+    fp(3)
+    jl(2)
+    v_ones = V([], "ms", T.ones[:], 1.0)
+    for b in ("E", "SG", "LS"):
+        v_one = V([], "ms", T[b][:], 1.0)
+    v_one = V([], "ms", T.NL[:], -1.0)
+    jl(3)
+    v_o1 = V([l_own], "ts", T.o1[:], T.owi[:], 1.0, None, A.add)
+    v_mk = V([], "ms", T.mk[:, 0:1024], 0.0)
+    v_x1 = V([v_o1], "ts", T.x1[:], T.o1[:], 1, None, A.arith_shift_right)
+    v_par = V([v_o1], "ts", T.par[:], T.o1[:], 1, None, A.bitwise_and)
+    v_cc = V([v_pm], "ts", T.ccol[:], T.pm[:], 16.0, None, A.mult)
+    v_xw = V([v_x1], "ts", T.XW[:], T.x1[:], 2.0, -4096.0, A.mult, A.add)
+    v_pc = V([v_par], "ts", T.parc[:], T.par[:], 1024.0, -2.0, A.mult, A.add)
+    v_cst = V([v_cc, c_ci], "ts", T.cst[:], T.ci[:], T.ccol[:], None, A.add)
+    v_b0 = V([v_pc, t_pts], "tt", T.base0[:], T.b7[:, 0:256], T.parc[:], A.add)
+
+    GRP = [[-16, 8], [0, 16]]
+    m = SEL([v_one], T.E[:], T.E[:], [[-16, 9], [0, 16]], A.is_ge, 0.0, 0, 1)
+    m = SEL([m], T.E[:], T.E[:], [[16, 9], [0, 16]], A.is_ge, 0.0, 15, -1)
+    m_e = SEL([m], T.E[:], T.E[:], [[0, 9], [1, 16]], A.is_equal, 0.0, -15, 0)
+    m = SEL([v_one], T.LS[:], T.LS[:], GRP, A.is_ge, 0.0, 0, 1)
+    m_ls = SEL([m], T.LS[:], T.LS[:], [[1, 128]], A.is_gt, 0.0, 0, -1)
+    m_b0 = rowsel(T.B0, [(0, 0.0625)])
+    m = SEL([v_one], T.SG[:], T.SG[:], GRP, A.is_ge, 0.0, 0, 1)
+    m_sg = SEL([m], T.SG[:], T.SG[:], [[16, 8], [0, 16]], A.is_ge, 0.0, 15, -1)
+    m = SEL([v_one], T.NL[:], T.NL[:], [[16, 8], [0, 16]], A.is_ge, 0.0, 15, -1)
+    m = SEL([m], T.NL[:], T.NL[:], [[-1, 128]], A.is_gt, 0.0, 0, 1)
+    m_nl = SEL([m], T.NL[:], T.NL[:], [[-1, 128]], A.not_equal, 0.5, 0, 1)
+
+    r_v = ("rv", 4 * len(eng))
+    g2 = [None] * 4
+    for q in (0, 2):
+        g2[q] = V([r_v, v_jl[q], v_zx], "cp", T.R2[:, 1024 * q:1024 * q + 1024],
+                  T.V2[:].indirect(T.jl[:, 64 * q:64 * q + 64]))
+    for q in (1, 3):
+        g2[q] = ACT([r_v, v_jl[q], v_zx], T.R2[:, 1024 * q:1024 * q + 1024],
+                    T.V2[:].indirect(T.jl[:, 64 * q:64 * q + 64]), F.Copy)
+    v_base = V([v_b0, t_fp[3]], "tt", T.base[:], T.b6[:, 0:256], T.base0[:], A.add)
+    v_e16 = V([m_e], "cp", T.E16[:], T.E[:])
+    v_e4k = V([m_e], "ts", T.E4k[:], T.E[:], 4096.0, None, A.mult)
+    t_k2 = [None] * 4
+    v_kept = [None] * 4
+    for q in range(4):
+        t_k2[q] = MM([g2[q], m_b2, v_jl[q]], rewrap(T["b%d" % q][:, 0:64], T.B2, T.R2, 64 * q, 64 * q + 64))
+        v_kept[q] = V([t_k2[q]], "ts", T.kept[:, 64 * q:64 * q + 64], T["b%d" % q][:, 0:64], 0.5, None, A.is_gt)
+        if q >= 1:
+            MM([v_kept[q - 1], m_e], [(T.b4[:, 0:16], T.E[:, 15 - s:143 - s], T.kept[:, 16 * s:16 * s + 16], s == 0, False)
+                                      for s in range(4 * q - 4, 4 * q)], False)
+    t_z = MM([v_kept[3], m_e], [(T.b4[:, 0:16], T.E[:, 15 - s:143 - s], T.kept[:, 16 * s:16 * s + 16], False, s == 15)
+                                for s in range(12, 16)])
+    v_zc = V([t_z, v_ones, v_zx], "scan", T.zx[:, 1:17], T.ones[:, 0:16], T.b4[:, 0:16], 0.0, A.mult, A.add)
+    t_off = MM([v_zc, m_ls], [(T.b5[:, 0:1], T.LS[:], T.zx[:, 16:17], True, True)])
+    v_e0 = V([t_z], "ts", T.e0[:], T.b4[:, 0:16], 0.0, None, A.is_equal)
+    v_e1 = V([v_e0, v_cst], "tt", T.e1[:], T.e0[:], T.cst[:], A.mult)
+    v_p1 = V([v_e1, v_zc], "tt", T.p1[:], T.e1[:], T.zx[:, 0:16], A.add)
+    v_zl = V([v_p1, t_off], "ts", T.zl[:], T.p1[:], T.b5[:, 0:1], None, A.add)
+    MM([m_sg, v_b0], [(T.b7[:, 0:256], T.SG[:], T.kept[:], True, True)])
+    t_n1 = MM([m_nl], [(T.b7[:, 256:512], T.NL[:], T.kept[:], True, True)])
+    v_mks = V([v_zl, v_mk, c_d3], "cp", T.mk[:].indirect(T.zl[:]), T.d3[:])
+    v_blk = V([v_mks], "scan", T.blk[:], T.mk[:, 0:1024], T.mk[:, 0:1024], 0.0, A.max, A.max)
+    t_bl = MM([v_blk, m_b0, v_zl], rewrap(T.b5[:, 64:128], T.B0, T.blk, 0, 64))
+    v_cum = V([t_n1], "scan", T.cum[:], T.ones[:], T.b7[:, 0:256], -1.5, A.mult, A.add)
+    v_kw = V([v_cum], "tt", T.KW[:], T.b7[:, 256:512], T.cum[:], A.add)
+    v_bl = V([t_bl], "cp", T.bl[:], T.b5[:, 64:128])
+    v_yw = None
+
+    def yw():
+        tok = None
+        for q in range(4):
+            tok = V([t_k2[q], v_base], "tt", T.YW[:, 64 * q:64 * q + 64], T["b%d" % q][:, 0:64],
+                    T.base[:, 64 * q:64 * q + 64], A.add)
+        return tok
+
+    t_x = t_y = None
+    for h in range(2):
+        m0, m1 = 512 * h, 512 * h + 512
+        bl = T.bl[:, 32 * h:32 * h + 32]
+        v_hit = V([v_kw, v_bl, c_mi], "tt", T.hit[:, m0:m1], T.KW[:].indirect(bl), T.mi[:, m0:m1], A.is_equal)
+        if h == 0:
+            v_yw = yw()
+        v_hx = V([v_hit, v_xw], "tt", T.hx[:, m0:m1], T.XW[:].indirect(bl), T.hit[:, m0:m1], A.mult)
+        v_hy = V([v_hit, v_yw], "tt", T.hy[:, m0:m1], T.YW[:].indirect(bl), T.hit[:, m0:m1], A.mult)
+        xs = range(8 * h, 8 * h + 8)
+        MM([v_hit, v_e4k, v_zc, v_e1], [(T.b4[:, 64:128], T.E4k[:, 15 - x:143 - x], T.hit[:, 64 * x:64 * x + 64], x == 0, False)
+                                  for x in xs], False)
+        t_x = MM([v_hx, v_e16], [(T.b4[:, 64:128], T.E16[:, 15 - x:143 - x], T.hx[:, 64 * x:64 * x + 64], False, x == 15)
+                                 for x in xs])
+        t_y = MM([v_hy, v_base], [(T.b6[:, 256:320], T.E16[:, 15 - x:143 - x], T.hy[:, 64 * x:64 * x + 64], x == 0, x == 15)
+                                  for x in xs])
+    v_pa = V([t_y], "ts", T.pa[:], T.b6[:, 256:320], 1023.5, -1.0, A.is_ge, A.add)
+    v_pm2 = V([t_y], "ts", T.pc[:], T.b6[:, 256:320], 1023.5, -1024.0, A.is_ge, A.mult)
+    v_ok = V([v_pa, t_x], "tt", T.ok[:], T.b4[:, 64:128], T.pa[:], A.add)
+    DMA("s", "dout", [v_ok], T.yk[:], T.ok[:])
+    v_os = V([v_pm2], "tt", T.osum[:], T.b6[:, 256:320], T.pc[:], A.add)
+    DMA("a", "dout", [v_os], T.ys[:], T.osum[:])
+    need("p", [(s, cnt[s]) for s in sorted(cnt)])

@@ -25,18 +25,17 @@ SCRATCH = {
     "pm": ("sbuf", [128, 1], "int32"),
     "hcol": ("sbuf", [128, 1], "float32"),
     "ccol": ("sbuf", [128, 1], "float32"),
+    "mcol": ("sbuf", [128, 1], "float32"),
     "ci": ("sbuf", [128, 16], "float32"),
     "cst": ("sbuf", [128, 16], "float32"),
-    "BI": ("sbuf", [128, 144], "bfloat16"),
-    "B2": ("sbuf", [128, 144], "bfloat16"),
-    "B0": ("sbuf", [128, 144], "bfloat16"),
-    "B8": ("sbuf", [128, 144], "bfloat16"),
-    "E": ("sbuf", [128, 144], "bfloat16"),
-    "E16": ("sbuf", [128, 144], "float16"),
-    "E4k": ("sbuf", [128, 144], "float16"),
-    "SG": ("sbuf", [128, 128], "bfloat16"),
-    "LS": ("sbuf", [128, 128], "bfloat16"),
+    "mc0": ("sbuf", [128, 64], "float32"),
+    "mcs": ("sbuf", [128, 64], "float32"),
+    "BZ": ("sbuf", [128, 704], "bfloat16"),
+    "BO": ("sbuf", [128, 400], "bfloat16"),
     "NL": ("sbuf", [128, 128], "bfloat16"),
+    "E16": ("sbuf", [128, 144], "float16"),
+    "I16": ("sbuf", [128, 128], "float16"),
+    "I4k": ("sbuf", [128, 128], "float16"),
     "ones": ("sbuf", [128, 256], "float32"),
     "d3": ("sbuf", [128, 256], "bfloat16"),
     "mi": ("sbuf", [128, 1024], "float32"),
@@ -49,6 +48,7 @@ SCRATCH = {
     "parc": ("sbuf", [128, 256], "float32"),
     "base0": ("sbuf", [128, 256], "float32"),
     "base": ("sbuf", [128, 256], "float32"),
+    "kT": ("sbuf", [128, 256], "bfloat16"),
     "kept": ("sbuf", [128, 256], "bfloat16"),
     "zx": ("sbuf", [128, 32], "bfloat16"),
     "e0": ("sbuf", [128, 16], "float32"),
@@ -59,9 +59,12 @@ SCRATCH = {
     "KW": ("sbuf", [128, 256], "float32"),
     "XW": ("sbuf", [128, 256], "float32"),
     "YW": ("sbuf", [128, 256], "float32"),
+    "gy": ("sbuf", [128, 512], "float16"),
     "hit": ("sbuf", [128, 1024], "float16"),
     "hx": ("sbuf", [128, 1024], "float16"),
     "hy": ("sbuf", [128, 1024], "float16"),
+    "F4": ("sbuf", [128, 64], "float32"),
+    "ox": ("sbuf", [128, 64], "float32"),
     "pa": ("sbuf", [128, 64], "float32"),
     "pc": ("sbuf", [128, 64], "float32"),
     "ok": ("sbuf", [128, 64], "float32"),
@@ -71,6 +74,10 @@ for _k in range(8):
     SCRATCH["b%d" % _k] = ("psum", [128, 512], "float32")
 SEMAPHORES = ["v", "a", "t", "p", "down", "dpts", "dnxt", "drow", "dpr", "dprow", "dout",
               "rown", "rpts", "rv", "sent"]
+
+NA = 136
+SUBS = [(k, k + 32) for k in range(0, 256, 32)]
+SENDS = [(0, 32), (32, 96), (96, 160), (160, 224), (224, 256)]
 
 
 def rank_program(g, core, T, topo):
@@ -118,18 +125,19 @@ def rank_program(g, core, T, topo):
             ins = q.tensor_tensor_scan(*args)
         return done("v", ins, 1)
 
-    def ACT(toks, out, in_, func):
+    def ACT(toks, out, in_, func, bias=None):
         need("a", toks)
-        return done("a", g.scalar.activation(out, in_, func), 1)
+        ins = g.scalar.activation(out, in_, func) if bias is None else g.scalar.activation(out, in_, func, bias=bias)
+        return done("a", ins, 1)
 
     def IOTA(toks, out, pattern, base, cm, small=True):
         need("p", toks)
         ins = g.iota(out, pattern, base, cm, allow_small_or_imprecise_dtypes=True) if small else g.iota(out, pattern, base, cm)
         return done("p", ins, 1)
 
-    def SEL(toks, out, in_, pattern, cmp, fill, base, cm):
+    def SEL(toks, buf, pattern, cmp, fill, base, cm):
         need("p", toks)
-        return done("p", g.affine_select(out, in_, pattern, cmp, fill, base, cm), 1)
+        return done("p", g.affine_select(buf, buf, pattern, cmp, fill, base, cm), 1)
 
     def DMA(q, s, toks, out, in_):
         need(q, toks)
@@ -150,8 +158,15 @@ def rank_program(g, core, T, topo):
         cnt["sent"] = cnt.get("sent", 0) + n
         cnt[sem] = cnt.get(sem, 0) + n
 
+    def moved(mat, t, K=128):
+        buf, c = mat
+        return buf[0:K, c + 15 - t:c + 143 - t]
+
     def rewrap(out, mat, src, c0, c1, K=128):
-        return [(out, mat[0:K, 15 - t:143 - t], src[0:K, 16 * c0 + t:16 * c1:16], t == 0, t == 15) for t in range(16)]
+        return [(out, moved(mat, t, K), src[0:K, 16 * c0 + t:16 * c1:16], t == 0, t == 15) for t in range(16)]
+
+    def el(buf, c0, c1):
+        return buf[:, 16 * c0:16 * c1]
 
     l_own = DMA("s", "down", [], T.owi[:], T.own[:])
     l_pts = DMA("a", "dpts", [], T.pti[:], T.pts[:])
@@ -163,7 +178,7 @@ def rank_program(g, core, T, topo):
     a1 = ACT([z0], T.WB[:, 512:1024], T.WB[:, 0:512], F.Silu)
     a2 = ACT([a1], T.D[:, 3072:4096], T.WB[:, 0:1024], F.Silu)
     a3 = ACT([a1], T.WB[:, 1024:2048], T.WB[:, 0:1024], F.Silu)
-    a4 = ACT([a3], T.WB[:, 2048:4096], T.WB[:, 0:2048], F.Silu)
+    ACT([a3], T.WB[:, 2048:4096], T.WB[:, 0:2048], F.Silu)
     a5 = ACT([a3], T.WB[:, 4096:6144], T.WB[:, 0:2048], F.Silu)
     V([], "ms", T.D[:, 0:2048], 0.0)
     v_pf = V([l_pts], "ts", T.pf[:], T.pti[:], 16.0, 16.0, A.mult, A.add)
@@ -179,40 +194,46 @@ def rank_program(g, core, T, topo):
     d_lh = DMA("s", "drow", [v_ht], T.D[0::16, :], T.ht[:])
     d_pr = DMA("s", "dpr", [r_pts], T.D[2::16, :], T.pf1[:])
 
-    p_z1 = IOTA([], T.WB[:, 6144:7168], [[0, 1024]], 0, 0)
+    IOTA([], T.WB[:, 6144:7168], [[0, 1024]], 0, 0)
     p_z2 = IOTA([], T.WB[:, 7168:8192], [[0, 1024]], 0, 0)
     v_wa = V([], "ms", T.WA[:], 0.0)
-    for b in ("BI", "B2", "B0", "B8"):
-        v_z = V([], "ms", T[b][:], 0.0)
+    v_z = V([], "ms", T.BZ[:], 0.0)
     V([], "ms", T.V2[:, 4096:4112], 0.0)
     v_zx = V([], "ms", T.zx[:], 0.0)
     v_nl = V([l_nxt], "cp", T.nl[:], T.nxi[:])
-    v_olb = V([r_own], "cp", T.ol[:, 128:256], T.own1[:, 128:256])
-    v_ola = V([], "cp", T.ol[:, 0:128], T.own1[:, 0:128])
+    v_olb = V([r_own], "cp", T.ol[:, NA:256], T.own1[:, NA:256])
+    v_ola = V([], "cp", T.ol[:, 0:NA], T.own1[:, 0:NA])
     v_pb = V([l_pts], "ts", T.pb[:], T.pti[:], 1.0, None, A.mult)
 
-    s_b = ACT([a5, p_z2, v_olb, d_lh, d_pr], T.WB[:].indirect(T.ol[:, 128:256]), T.D[:, 2048:4096], F.Silu)
-    s_a = V([v_wa, v_ola, d_lh, d_pr], "cp", T.WA[:].indirect(T.ol[:, 0:128]), T.D[:, 0:2048])
+    s_b = ACT([a5, p_z2, v_olb, d_lh, d_pr], T.WB[:].indirect(T.ol[:, NA:256]), el(T.D, NA, 256), F.Silu)
+    s_a = V([v_wa, v_ola, d_lh, d_pr], "cp", T.WA[:].indirect(T.ol[:, 0:NA]), el(T.D, 0, NA))
     d_prow = DMA("s", "dprow", [v_pb], T.prow[:], T.pb[:])
 
-    def rowsel(buf, fills):
+    BI, B2, B0, B8 = ((T.BZ, 144 * k) for k in range(4))
+    ID = T.BZ[:, 576:704]
+    E = (T.BO, 0)
+    LS = T.BO[:, 144:272]
+    SG = T.BO[:, 272:400]
+
+    def rowsel(mat, fills):
+        buf = mat[0][:, mat[1]:mat[1] + 144]
         tok = v_z
         for k, w in fills:
-            tok = SEL([tok], buf[:], buf[:], [[-16, 9], [0, 16]], A.not_equal, w, -k, 1)
-        return SEL([tok], buf[:], buf[:], [[0, 9], [1, 16]], A.is_equal, 0.0, -15, 0)
+            tok = SEL([tok], buf, [[-16, 9], [0, 16]], A.not_equal, w, -k, 1)
+        return SEL([tok], buf, [[0, 9], [1, 16]], A.is_equal, 0.0, -15, 0)
 
-    m_bi = rowsel(T.BI, [(0, 16.0), (1, 0.0625)])
-    m_b2 = rowsel(T.B2, [(2, 0.0625)])
-    m_b8 = SEL([v_z], T.B8[:], T.B8[:], [[-1, 144]], A.not_equal, 1.0, 15, 16)
+    m_bi = rowsel(BI, [(0, 16.0), (1, 0.0625)])
+    m_b2 = rowsel(B2, [(2, 0.0625)])
+    m_b8 = SEL([v_z], T.BZ[:, 432:576], [[-1, 144]], A.not_equal, 1.0, 15, 16)
     c_d3 = IOTA([], T.d3[:], [[16, 16], [256, 16]], 0, 0)
     c_ci = IOTA([], T.ci[:], [[1, 16]], 1025, 0)
-    c_mi = IOTA([], T.mi[:], [[1, 1024]], 0, 0)
+    c_mc = IOTA([], T.mc0[:], [[1, 64]], 0, 0)
+    m_id = SEL([v_z], ID, [[-1, 128]], A.not_equal, 1.0, 0, 1)
 
-    t_pts = MM([m_b8, d_prow], rewrap(T.b7[:, 0:256], T.B8, T.prow, 0, 256, 8))
+    t_pts = MM([m_b8, d_prow], rewrap(T.b7[:, 0:256], B8, T.prow, 0, 256, 8))
 
-    subs = [(k * 32, k * 32 + 32) for k in range(8)]
-    g_a = [ACT([s_b, v_nl], T.bg[:, 16 * c0:16 * c1], T.WB[:].indirect(T.nl[:, c0:c1]), F.Copy) for c0, c1 in subs]
-    g_v = [None] * 4
+    g_a = [ACT([s_b, v_nl], el(T.bg, c0, c1), T.WB[:].indirect(T.nl[:, c0:c1]), F.Copy) for c0, c1 in SUBS]
+    upto = {}
     t_code = [None] * 4
     t_fp = [None] * 4
     v_jl = [None] * 4
@@ -221,113 +242,143 @@ def rank_program(g, core, T, topo):
         v_jl[q] = V([t_code[q]], "ts", T.jl[:, 64 * q:64 * q + 64], T["b%d" % q][:, 0:64], -1.0, 4096.0, A.mult, A.add)
 
     def fp(q):
-        t_fp[q] = MM([g_v[q], m_b2], rewrap(T.b6[:, 64 * q:64 * q + 64], T.B2, T.R, 64 * q, 64 * q + 64))
+        t_fp[q] = MM([upto[64 * q + 64], m_b2], rewrap(T.b6[:, 64 * q:64 * q + 64], B2, T.R, 64 * q, 64 * q + 64))
 
-    for q in range(4):
-        for k in (2 * q, 2 * q + 1):
-            c0, c1 = subs[k]
-            g_v[q] = V([s_a, g_a[k], v_nl], "tt", T.R[:, 16 * c0:16 * c1], T.WA[:].indirect(T.nl[:, c0:c1]),
-                       T.bg[:, 16 * c0:16 * c1], A.add)
-        SEND([g_v[q]], T.V2[:, 1024 * q:1024 * q + 1024], T.R[:, 1024 * q:1024 * q + 1024], "rv", mask)
-        t_code[q] = MM([g_v[q], m_bi], rewrap(T["b%d" % q][:, 0:64], T.BI, T.R, 64 * q, 64 * q + 64))
-        if q >= 1:
-            fp(q - 1)
-        if q >= 2:
-            jl(q - 2)
-    fp(3)
-    jl(2)
-    v_ones = V([], "ms", T.ones[:], 1.0)
-    for b in ("E", "SG", "LS"):
-        v_one = V([], "ms", T[b][:], 1.0)
-    v_one = V([], "ms", T.NL[:], -1.0)
-    jl(3)
+    for k, (c0, c1) in enumerate(SUBS):
+        upto[c1] = V([s_a, g_a[k], v_nl], "tt", el(T.R, c0, c1), T.WA[:].indirect(T.nl[:, c0:c1]), el(T.bg, c0, c1), A.add)
+        for s0, s1 in SENDS:
+            if s1 == c1:
+                SEND([upto[c1]], el(T.V2, s0, s1), el(T.R, s0, s1), "rv", mask)
+        if c1 % 64 == 0:
+            q = c1 // 64 - 1
+            t_code[q] = MM([upto[c1], m_bi], rewrap(T["b%d" % q][:, 0:64], BI, T.R, 64 * q, 64 * q + 64))
+            if q == 1:
+                fp(0)
+            if q >= 2:
+                jl(q - 2)
+    fp(1)
+    fp(2)
+    v_one = V([], "ms", T.BO[:], 1.0)
+    v_neg = V([], "ms", T.NL[:], -1.0)
     v_o1 = V([l_own], "ts", T.o1[:], T.owi[:], 1.0, None, A.add)
-    v_mk = V([], "ms", T.mk[:, 0:1024], 0.0)
+    v_cc = V([v_pm], "ts", T.ccol[:], T.pm[:], 16.0, None, A.mult)
+    v_mcol = V([], "ts", T.mcol[:], T.pm[:], 64.0, -0.75, A.mult, A.add)
+    jl(2)
     v_x1 = V([v_o1], "ts", T.x1[:], T.o1[:], 1, None, A.arith_shift_right)
     v_par = V([v_o1], "ts", T.par[:], T.o1[:], 1, None, A.bitwise_and)
-    v_cc = V([v_pm], "ts", T.ccol[:], T.pm[:], 16.0, None, A.mult)
     v_xw = V([v_x1], "ts", T.XW[:], T.x1[:], 2.0, -4096.0, A.mult, A.add)
     v_pc = V([v_par], "ts", T.parc[:], T.par[:], 1024.0, -2.0, A.mult, A.add)
+    jl(3)
+    c_mk = V([], "ms", T.mk[:, 0:1024], 0.0)
+    c_ones = V([], "ms", T.ones[:], 1.0)
     v_cst = V([v_cc, c_ci], "ts", T.cst[:], T.ci[:], T.ccol[:], None, A.add)
-    v_b0 = V([v_pc, t_pts], "tt", T.base0[:], T.b7[:, 0:256], T.parc[:], A.add)
+    v_mc = V([v_mcol, c_mc], "ts", T.mcs[:], T.mc0[:], T.mcol[:], None, A.add)
 
     GRP = [[-16, 8], [0, 16]]
-    m = SEL([v_one], T.E[:], T.E[:], [[-16, 9], [0, 16]], A.is_ge, 0.0, 0, 1)
-    m = SEL([m], T.E[:], T.E[:], [[16, 9], [0, 16]], A.is_ge, 0.0, 15, -1)
-    m_e = SEL([m], T.E[:], T.E[:], [[0, 9], [1, 16]], A.is_equal, 0.0, -15, 0)
-    m = SEL([v_one], T.LS[:], T.LS[:], GRP, A.is_ge, 0.0, 0, 1)
-    m_ls = SEL([m], T.LS[:], T.LS[:], [[1, 128]], A.is_gt, 0.0, 0, -1)
-    m_b0 = rowsel(T.B0, [(0, 0.0625)])
-    m = SEL([v_one], T.SG[:], T.SG[:], GRP, A.is_ge, 0.0, 0, 1)
-    m_sg = SEL([m], T.SG[:], T.SG[:], [[16, 8], [0, 16]], A.is_ge, 0.0, 15, -1)
-    m = SEL([v_one], T.NL[:], T.NL[:], [[16, 8], [0, 16]], A.is_ge, 0.0, 15, -1)
-    m = SEL([m], T.NL[:], T.NL[:], [[-1, 128]], A.is_gt, 0.0, 0, 1)
-    m_nl = SEL([m], T.NL[:], T.NL[:], [[-1, 128]], A.not_equal, 0.5, 0, 1)
+    PRG = [[16, 8], [0, 16]]
+    m = SEL([v_one], T.BO[:, 0:144], [[-16, 9], [0, 16]], A.is_ge, 0.0, 0, 1)
+    m = SEL([m], T.BO[:, 0:144], [[16, 9], [0, 16]], A.is_ge, 0.0, 15, -1)
+    m_e = SEL([m], T.BO[:, 0:144], [[0, 9], [1, 16]], A.is_equal, 0.0, -15, 0)
+    m = SEL([v_one], LS, GRP, A.is_ge, 0.0, 0, 1)
+    m_ls = SEL([m], LS, [[1, 128]], A.is_gt, 0.0, 0, -1)
+    m = SEL([v_one], SG, GRP, A.is_ge, 0.0, 0, 1)
+    m_sg = SEL([m], SG, PRG, A.is_ge, 0.0, 15, -1)
+    m = SEL([v_neg], T.NL[:], PRG, A.is_ge, 0.0, 15, -1)
+    m = SEL([m], T.NL[:], [[-1, 128]], A.is_gt, 0.0, 0, 1)
+    m_nl = SEL([m], T.NL[:], [[-1, 128]], A.not_equal, 0.5, 0, 1)
+    m_b0 = rowsel(B0, [(0, 0.0625)])
+    c_mi = IOTA([], T.mi[:], [[1, 1024]], 0, 0)
 
-    r_v = ("rv", 4 * len(eng))
-    g2 = [None] * 4
-    for q in (0, 2):
-        g2[q] = V([r_v, v_jl[q], v_zx], "cp", T.R2[:, 1024 * q:1024 * q + 1024],
-                  T.V2[:].indirect(T.jl[:, 64 * q:64 * q + 64]))
-    for q in (1, 3):
-        g2[q] = ACT([r_v, v_jl[q], v_zx], T.R2[:, 1024 * q:1024 * q + 1024],
-                    T.V2[:].indirect(T.jl[:, 64 * q:64 * q + 64]), F.Copy)
-    v_base = V([v_b0, t_fp[3]], "tt", T.base[:], T.b6[:, 0:256], T.base0[:], A.add)
-    v_e16 = V([m_e], "cp", T.E16[:], T.E[:])
-    v_e4k = V([m_e], "ts", T.E4k[:], T.E[:], 4096.0, None, A.mult)
-    t_k2 = [None] * 4
-    v_kept = [None] * 4
+    r_v = ("rv", len(SENDS) * len(eng))
+    g2 = []
     for q in range(4):
-        t_k2[q] = MM([g2[q], m_b2, v_jl[q]], rewrap(T["b%d" % q][:, 0:64], T.B2, T.R2, 64 * q, 64 * q + 64))
-        v_kept[q] = V([t_k2[q]], "ts", T.kept[:, 64 * q:64 * q + 64], T["b%d" % q][:, 0:64], 0.5, None, A.is_gt)
-        if q >= 1:
-            MM([v_kept[q - 1], m_e], [(T.b4[:, 0:16], T.E[:, 15 - s:143 - s], T.kept[:, 16 * s:16 * s + 16], s == 0, False)
-                                      for s in range(4 * q - 4, 4 * q)], False)
-    t_z = MM([v_kept[3], m_e], [(T.b4[:, 0:16], T.E[:, 15 - s:143 - s], T.kept[:, 16 * s:16 * s + 16], False, s == 15)
-                                for s in range(12, 16)])
-    v_zc = V([t_z, v_ones, v_zx], "scan", T.zx[:, 1:17], T.ones[:, 0:16], T.b4[:, 0:16], 0.0, A.mult, A.add)
-    t_off = MM([v_zc, m_ls], [(T.b5[:, 0:1], T.LS[:], T.zx[:, 16:17], True, True)])
+        c0, cm, c1 = 64 * q, 64 * q + 32, 64 * q + 64
+        g2.append(V([r_v, v_jl[q], v_zx], "cp", el(T.R2, c0, cm), T.V2[:].indirect(T.jl[:, c0:cm])))
+        g2.append(ACT([r_v, v_jl[q], v_zx], el(T.R2, cm, c1), T.V2[:].indirect(T.jl[:, cm:c1]), F.Copy))
+
+    def kt(h):
+        return [(T["b%d" % h][:, t:128:16], T.R2[:, 2048 * h + t:2048 * h + 2048:16], T.BZ[:, 159:287:16], True, True)
+                for t in range(16)]
+
+    def evac(h, tok):
+        return V([tok], "cp", T.kT[:, 128 * h:128 * h + 128], T["b%d" % h][:, 0:128])
+
+    def back(h, tok):
+        return MM([tok, m_id], [(T["b%d" % (2 + h)][:, 0:128], T.kT[:, 128 * h:128 * h + 128], ID, True, True)])
+
+    def kept(h, tok):
+        return V([tok], "ts", T.kept[:, 128 * h:128 * h + 128], T["b%d" % (2 + h)][:, 0:128], 0.5, None, A.is_gt)
+
+    def zsum(s0, s1):
+        return [(T.b4[:, 0:16], moved(E, s), T.kept[:, 16 * s:16 * s + 16], s == 0, s == 15) for s in range(s0, s1)]
+
+    t_kt0 = MM(g2[:4] + [m_b2] + v_jl, kt(0))
+    v_t0 = evac(0, t_kt0)
+    kt1 = kt(1)
+    MM(g2[4:], kt1[:8], False)
+    t_k0 = back(0, v_t0)
+    t_kt1 = MM([], kt1[8:])
+    v_k0 = kept(0, t_k0)
+    v_t1 = evac(1, t_kt1)
+    MM([v_k0, m_e], zsum(0, 4), False)
+    t_k1 = back(1, v_t1)
+    MM([], zsum(4, 8), False)
+    v_k1 = kept(1, t_k1)
+    t_z = MM([v_k1], zsum(8, 16))
+    t_k2 = [t_k0, t_k1]
+    v_b0 = V([v_pc, t_pts], "tt", T.base0[:], T.b7[:, 0:256], T.parc[:], A.add)
+    v_e16 = V([m_e], "cp", T.E16[:], T.BO[:, 0:144])
+    V([m_id], "cp", T.I16[:], ID)
+    v_i4k = V([], "ts", T.I4k[:], ID, 4096.0, None, A.mult)
+    v_zc = V([t_z, c_ones, v_zx], "scan", T.zx[:, 1:17], T.ones[:, 0:16], T.b4[:, 0:16], 0.0, A.mult, A.add)
+    t_off = MM([v_zc, m_ls], [(T.b5[:, 0:1], LS, T.zx[:, 16:17], True, True)])
     v_e0 = V([t_z], "ts", T.e0[:], T.b4[:, 0:16], 0.0, None, A.is_equal)
     v_e1 = V([v_e0, v_cst], "tt", T.e1[:], T.e0[:], T.cst[:], A.mult)
     v_p1 = V([v_e1, v_zc], "tt", T.p1[:], T.e1[:], T.zx[:, 0:16], A.add)
     v_zl = V([v_p1, t_off], "ts", T.zl[:], T.p1[:], T.b5[:, 0:1], None, A.add)
-    MM([m_sg, v_b0], [(T.b7[:, 0:256], T.SG[:], T.kept[:], True, True)])
+    MM([m_sg, v_b0], [(T.b7[:, 0:256], SG, T.kept[:], True, True)])
     t_n1 = MM([m_nl], [(T.b7[:, 256:512], T.NL[:], T.kept[:], True, True)])
-    v_mks = V([v_zl, v_mk, c_d3], "cp", T.mk[:].indirect(T.zl[:]), T.d3[:])
+    fp(3)
+    v_mks = V([v_zl, c_mk, c_d3], "cp", T.mk[:].indirect(T.zl[:]), T.d3[:])
     v_blk = V([v_mks], "scan", T.blk[:], T.mk[:, 0:1024], T.mk[:, 0:1024], 0.0, A.max, A.max)
-    t_bl = MM([v_blk, m_b0, v_zl], rewrap(T.b5[:, 64:128], T.B0, T.blk, 0, 64))
+    t_bl = MM([v_blk, m_b0, v_zl], rewrap(T.b5[:, 64:128], B0, T.blk, 0, 64))
     v_cum = V([t_n1], "scan", T.cum[:], T.ones[:], T.b7[:, 0:256], -1.5, A.mult, A.add)
+    v_base = V([v_b0, t_fp[3]], "tt", T.base[:], T.b6[:, 0:256], T.base0[:], A.add)
     v_kw = V([v_cum], "tt", T.KW[:], T.b7[:, 256:512], T.cum[:], A.add)
-    v_bl = V([t_bl], "cp", T.bl[:], T.b5[:, 64:128])
     v_yw = None
-
-    def yw():
-        tok = None
-        for q in range(4):
-            tok = V([t_k2[q], v_base], "tt", T.YW[:, 64 * q:64 * q + 64], T["b%d" % q][:, 0:64],
-                    T.base[:, 64 * q:64 * q + 64], A.add)
-        return tok
-
-    t_x = t_y = None
     for h in range(2):
-        m0, m1 = 512 * h, 512 * h + 512
-        bl = T.bl[:, 32 * h:32 * h + 32]
-        v_hit = V([v_kw, v_bl, c_mi], "tt", T.hit[:, m0:m1], T.KW[:].indirect(bl), T.mi[:, m0:m1], A.is_equal)
-        if h == 0:
-            v_yw = yw()
-        v_hx = V([v_hit, v_xw], "tt", T.hx[:, m0:m1], T.XW[:].indirect(bl), T.hit[:, m0:m1], A.mult)
-        v_hy = V([v_hit, v_yw], "tt", T.hy[:, m0:m1], T.YW[:].indirect(bl), T.hit[:, m0:m1], A.mult)
-        xs = range(8 * h, 8 * h + 8)
-        MM([v_hit, v_e4k, v_zc, v_e1], [(T.b4[:, 64:128], T.E4k[:, 15 - x:143 - x], T.hit[:, 64 * x:64 * x + 64], x == 0, False)
-                                  for x in xs], False)
-        t_x = MM([v_hx, v_e16], [(T.b4[:, 64:128], T.E16[:, 15 - x:143 - x], T.hx[:, 64 * x:64 * x + 64], False, x == 15)
-                                 for x in xs])
-        t_y = MM([v_hy, v_base], [(T.b6[:, 256:320], T.E16[:, 15 - x:143 - x], T.hy[:, 64 * x:64 * x + 64], x == 0, x == 15)
-                                  for x in xs])
-    v_pa = V([t_y], "ts", T.pa[:], T.b6[:, 256:320], 1023.5, -1.0, A.is_ge, A.add)
-    v_pm2 = V([t_y], "ts", T.pc[:], T.b6[:, 256:320], 1023.5, -1024.0, A.is_ge, A.mult)
-    v_ok = V([v_pa, t_x], "tt", T.ok[:], T.b4[:, 64:128], T.pa[:], A.add)
+        c0, c1 = 128 * h, 128 * h + 128
+        v_yw = V([t_k2[h], v_base], "tt", T.YW[:, c0:c1], T["b%d" % (2 + h)][:, 0:128], T.base[:, c0:c1], A.add)
+    v_bl = V([t_bl], "cp", T.bl[:], T.b5[:, 64:128])
+
+    def osum(dst, src, xs, first, last):
+        return [(dst, T.E16[:, 15 - x:143 - x], src[:, 64 * x:64 * x + 64], first and x == xs[0], last and x == xs[-1])
+                for x in xs]
+
+    PX, PY = T.b4[:, 64:128], T.b6[:, 256:320]
+    bl = [T.bl[:, 0:32], T.bl[:, 32:64]]
+    hs = [(0, 512), (512, 1024)]
+    a_gy = ACT([v_yw, v_bl], T.gy[:], T.YW[:].indirect(bl[0]), F.Copy)
+    v_hit = [V([v_kw, v_bl, c_mi], "tt", T.hit[:, m0:m1], T.KW[:].indirect(bl[h]), T.mi[:, m0:m1], A.is_equal)
+             for h, (m0, m1) in enumerate(hs)]
+    v_hx = [V([v_hit[h], v_xw], "tt", T.hx[:, m0:m1], T.XW[:].indirect(bl[h]), T.hit[:, m0:m1], A.mult)
+            for h, (m0, m1) in enumerate(hs)]
+    v_f = V([v_mc, v_cum], "ts", T.F4[:], T.mcs[:], T.cum[:, 255:256], 4096.0, A.is_le, A.mult)
+    v_hy = [V([v_hit[1], v_yw], "tt", T.hy[:, n:n + 256], T.YW[:].indirect(T.bl[:, n // 16:n // 16 + 16]), T.hit[:, n:n + 256],
+              A.mult) for n in (512, 768)]
+    MM([a_gy, v_i4k], [(T.b0[:], T.I16[:], T.gy[:], True, False)], False)
+    t_m = MM([v_hit[0]], [(T.b0[:], T.I4k[:], T.hit[:, 0:512], False, True)])
+    a_hy = ACT([t_m], T.hy[:, 0:512], T.b0[:], F.Relu, -4096.0)
+    MM([v_hx[0], v_e16, v_zc, v_e1], osum(PX, T.hx, range(0, 8), True, False), False)
+    MM([a_hy, v_base], osum(PY, T.hy, range(0, 8), True, False), False)
+    t_x = MM([v_hx[1]], osum(PX, T.hx, range(8, 16), False, True))
+    MM([v_hy[0]], osum(PY, T.hy, range(8, 12), False, False), False)
+    t_y = MM([v_hy[1]], osum(PY, T.hy, range(12, 16), False, True))
+    v_ox = V([v_f, t_x], "tt", T.ox[:], PX, T.F4[:], A.add)
+    v_pa = V([t_y], "ts", T.pa[:], PY, 1023.5, -1.0, A.is_ge, A.add)
+    v_pm2 = V([], "ts", T.pc[:], PY, 1023.5, -1024.0, A.is_ge, A.mult)
+    v_ok = V([v_pa, v_ox], "tt", T.ok[:], T.ox[:], T.pa[:], A.add)
     DMA("s", "dout", [v_ok], T.yk[:], T.ok[:])
-    v_os = V([v_pm2], "tt", T.osum[:], T.b6[:, 256:320], T.pc[:], A.add)
+    v_os = V([v_pm2], "tt", T.osum[:], PY, T.pc[:], A.add)
     DMA("a", "dout", [v_os], T.ys[:], T.osum[:])
     need("p", [(s, cnt[s]) for s in sorted(cnt)])

@@ -4,26 +4,32 @@ SCRATCH = {
     "owi": ("sbuf", [128, 256], "int32"),
     "pti": ("sbuf", [128, 256], "int32"),
     "nxi": ("sbuf", [128, 256], "int32"),
-    "pf": ("sbuf", [128, 256], "float32"),
-    "pb": ("sbuf", [128, 256], "bfloat16"),
-    "own1": ("sbuf", [128, 256], "int32"),
-    "pf1": ("sbuf", [128, 256], "float32"),
-    "ol": ("sbuf", [128, 256], "uint16"),
+    "nls": ("sbuf", [128, 256], "uint16"),
     "nl": ("sbuf", [128, 256], "uint16"),
+    "pb": ("sbuf", [128, 256], "bfloat16"),
+    "pfB": ("sbuf", [128, 128], "float32"),
+    "ltA": ("sbuf", [128, 128], "bfloat16"),
+    "htA": ("sbuf", [128, 128], "bfloat16"),
+    "ltB": ("sbuf", [128, 128], "float32"),
+    "htB": ("sbuf", [128, 128], "float32"),
+    "ol": ("sbuf", [128, 256], "uint16"),
     "jl": ("sbuf", [128, 256], "uint16"),
-    "D": ("sbuf", [128, 4096], "float32"),
+    "jy": ("sbuf", [128, 96], "uint16"),
+    "jx": ("sbuf", [128, 160], "uint16"),
+    "DA": ("sbuf", [128, 2048], "bfloat16"),
+    "DB": ("sbuf", [128, 2048], "float32"),
     "WA": ("sbuf", [128, 8192], "bfloat16"),
     "WB": ("sbuf", [128, 8192], "float32"),
     "bg": ("sbuf", [128, 4096], "bfloat16"),
-    "R": ("sbuf", [128, 4096], "bfloat16"),
+    "R": ("sbuf", [128, 4112], "bfloat16"),
     "V2": ("sbuf", [128, 4112], "bfloat16"),
-    "R2": ("sbuf", [128, 4096], "bfloat16"),
+    "R2y": ("sbuf", [128, 1536], "bfloat16"),
+    "R2x": ("sbuf", [128, 2560], "bfloat16"),
     "prow": ("sbuf", [8, 4096], "bfloat16"),
-    "lt": ("sbuf", [128, 256], "float32"),
-    "ht": ("sbuf", [128, 256], "float32"),
     "pid": ("sbuf", [128, 1], "int32"),
     "pm": ("sbuf", [128, 1], "int32"),
-    "hcol": ("sbuf", [128, 1], "float32"),
+    "hA": ("sbuf", [128, 1], "float32"),
+    "hB": ("sbuf", [128, 1], "float32"),
     "ccol": ("sbuf", [128, 1], "float32"),
     "mcol": ("sbuf", [128, 1], "float32"),
     "ci": ("sbuf", [128, 16], "float32"),
@@ -45,10 +51,13 @@ SCRATCH = {
     "o1": ("sbuf", [128, 256], "int32"),
     "x1": ("sbuf", [128, 256], "int32"),
     "par": ("sbuf", [128, 256], "int32"),
-    "parc": ("sbuf", [128, 256], "float32"),
-    "base0": ("sbuf", [128, 256], "float32"),
-    "base": ("sbuf", [128, 256], "float32"),
-    "kT": ("sbuf", [128, 256], "bfloat16"),
+    "parb": ("sbuf", [128, 256], "bfloat16"),
+    "kYs": ("sbuf", [128, 128], "bfloat16"),
+    "kYl": ("sbuf", [128, 128], "bfloat16"),
+    "kX1": ("sbuf", [128, 128], "bfloat16"),
+    "kX2": ("sbuf", [32, 128], "bfloat16"),
+    "kfs": ("sbuf", [128, 256], "bfloat16"),
+    "kfl": ("sbuf", [128, 256], "bfloat16"),
     "kept": ("sbuf", [128, 256], "bfloat16"),
     "zx": ("sbuf", [128, 32], "bfloat16"),
     "e0": ("sbuf", [128, 16], "float32"),
@@ -59,7 +68,7 @@ SCRATCH = {
     "KW": ("sbuf", [128, 256], "float32"),
     "XW": ("sbuf", [128, 256], "float32"),
     "YW": ("sbuf", [128, 256], "float32"),
-    "gy": ("sbuf", [128, 512], "float16"),
+    "gy": ("sbuf", [128, 640], "float16"),
     "hit": ("sbuf", [128, 1024], "float16"),
     "hx": ("sbuf", [128, 1024], "float16"),
     "hy": ("sbuf", [128, 1024], "float16"),
@@ -72,25 +81,19 @@ SCRATCH = {
 }
 for _k in range(8):
     SCRATCH["b%d" % _k] = ("psum", [128, 512], "float32")
-SEMAPHORES = ["v", "a", "t", "p", "down", "dpts", "dnxt", "drow", "dpr", "dprow", "dout",
-              "rown", "rpts", "rv", "sent"]
+SEMAPHORES = ["v", "a", "t", "p", "down", "dpts", "dnxt", "dda", "ddb", "dprow", "dout",
+              "rn", "rv", "ry0", "ry1", "rx0", "rx1", "rk", "rf", "sent"]
 
-NA = 136
-SUBS = [(k, k + 32) for k in range(0, 256, 32)]
+SUBS = [(0, 16), (16, 32)] + [(k, k + 32) for k in range(32, 224, 32)] + [(224, 240), (240, 256)]
 SENDS = [(0, 32), (32, 96), (96, 160), (160, 224), (224, 256)]
+NY = 96
 
 
 def rank_program(g, core, T, topo):
     rank = T.rank_of(core)
     if rank is None:
         return
-    prev = T.cores[(rank - 1) % 4]
-    rid, pid, _se = topo.addr(prev)
-    eng = topo.engines(core, prev)
-    half = len(eng) // 2
-    maskA = sum(1 << e for e in eng[:half])
-    maskB = sum(1 << e for e in eng[half:])
-    mask = topo.mask(core, prev)
+    prv, nxc, opp = (T.cores[(rank + k) % 4] for k in (3, 1, 2))
     queues = {"v": g.vector, "a": g.scalar, "t": g.tensor, "p": g, "s": g.sync}
     cnt = {}
     seen = {}
@@ -125,9 +128,14 @@ def rank_program(g, core, T, topo):
             ins = q.tensor_tensor_scan(*args)
         return done("v", ins, 1)
 
-    def ACT(toks, out, in_, func, bias=None):
+    def ACT(toks, out, in_, func, bias=None, scale=None):
         need("a", toks)
-        ins = g.scalar.activation(out, in_, func) if bias is None else g.scalar.activation(out, in_, func, bias=bias)
+        if scale is not None:
+            ins = g.scalar.activation(out, in_, func, scale=scale)
+        elif bias is not None:
+            ins = g.scalar.activation(out, in_, func, bias=bias)
+        else:
+            ins = g.scalar.activation(out, in_, func)
         return done("a", ins, 1)
 
     def IOTA(toks, out, pattern, base, cm, small=True):
@@ -150,205 +158,234 @@ def rank_program(g, core, T, topo):
             ins = g.tensor.matmul(out, lhs, rhs, st, sp)
         return done("t", ins, 1) if tok else None
 
-    def SEND(toks, dst, src, sem, m):
+    def SEND(toks, to, dst, src, sem):
         need("p", toks)
+        rid, pid, _se = topo.addr(to)
         g.remote_dma(out_ap=dst, in_ap=src, remote_sem=T.sem[sem], local_sem=T.sem.sent, pid=pid, routing_id=rid,
-                     dma_engine_mask=m)
-        n = bin(m).count("1")
+                     dma_engine_mask=topo.mask(core, to))
+        n = len(topo.engines(core, to))
         cnt["sent"] = cnt.get("sent", 0) + n
         cnt[sem] = cnt.get(sem, 0) + n
+        return (sem, cnt[sem])
 
     def moved(mat, t, K=128):
         buf, c = mat
         return buf[0:K, c + 15 - t:c + 143 - t]
 
-    def rewrap(out, mat, src, c0, c1, K=128):
-        return [(out, moved(mat, t, K), src[0:K, 16 * c0 + t:16 * c1:16], t == 0, t == 15) for t in range(16)]
+    def rewrap(out, mat, src, c0, c1, K=128, close=True):
+        return [(out, moved(mat, t, K), src[0:K, 16 * c0 + t:16 * c1:16], t == 0, close and t == 15) for t in range(16)]
 
     def el(buf, c0, c1):
         return buf[:, 16 * c0:16 * c1]
 
     l_own = DMA("s", "down", [], T.owi[:], T.own[:])
-    l_pts = DMA("a", "dpts", [], T.pti[:], T.pts[:])
+    DMA("a", "dpts", [], T.pti[:, 0:128], T.pts[:, 0:2048])
+    l_pts = DMA("a", "dpts", [], T.pti[:, 128:256], T.pts[:, 2048:4096])
     l_nxt = DMA("s", "dnxt", [], T.nxi[:], T.nxt[:])
 
     c_pid = IOTA([], T.pid[:], [[1, 1]], 0, 1, False)
-    c_lt = IOTA([], T.lt[:], [[-16, 256]], 4096, 0)
-    z0 = V([], "ms", T.WB[:, 0:512], 0.0)
-    a1 = ACT([z0], T.WB[:, 512:1024], T.WB[:, 0:512], F.Silu)
-    a2 = ACT([a1], T.D[:, 3072:4096], T.WB[:, 0:1024], F.Silu)
-    a3 = ACT([a1], T.WB[:, 1024:2048], T.WB[:, 0:1024], F.Silu)
+    c_lta = IOTA([], T.ltA[:], [[-16, 128]], 2048, 0)
+    c_ltb = IOTA([], T.ltB[:], [[-16, 128]], 2048, 0)
+    z0 = V([], "ms", T.WB[:, 0:128], 0.0)
+    v_da = V([], "ms", T.DA[:], 0.0)
+    z1 = V([], "ms", T.WB[:, 256:1024], 0.0)
+    v_db = V([], "ms", T.DB[:, 0:768], 0.0)
+    a1 = ACT([z0], T.WB[:, 128:256], T.WB[:, 0:128], F.Silu)
+    ACT([a1, z1], T.DB[:, 768:1792], T.WB[:, 0:1024], F.Silu)
+    a2 = ACT([], T.DB[:, 1792:2048], T.WB[:, 0:256], F.Silu)
+    a3 = ACT([], T.WB[:, 1024:2048], T.WB[:, 0:1024], F.Silu)
     ACT([a3], T.WB[:, 2048:4096], T.WB[:, 0:2048], F.Silu)
-    a5 = ACT([a3], T.WB[:, 4096:6144], T.WB[:, 0:2048], F.Silu)
-    V([], "ms", T.D[:, 0:2048], 0.0)
-    v_pf = V([l_pts], "ts", T.pf[:], T.pti[:], 16.0, 16.0, A.mult, A.add)
+    a5 = ACT([a3], T.WB[:, 4096:5632], T.WB[:, 0:1536], F.Silu)
     v_pm = V([c_pid], "ts", T.pm[:], T.pid[:], 15, None, A.bitwise_and)
-    v_d = V([], "ms", T.D[:, 2048:3072], 0.0)
-    v_h = V([v_pm], "ts", T.hcol[:], T.pm[:], -16.0, 240.0, A.mult, A.add)
-    v_ht = V([v_h, c_lt], "ts", T.ht[:], T.lt[:], 0.0, T.hcol[:], A.mult, A.add)
-    SEND([l_own], T.own1[:], T.owi[:], "rown", maskA)
-    SEND([v_pf], T.pf1[:], T.pf[:], "rpts", maskB)
-    r_own = ("rown", half)
-    r_pts = ("rpts", half)
-    DMA("s", "drow", [v_d, a2, c_lt], T.D[1::16, :], T.lt[:])
-    d_lh = DMA("s", "drow", [v_ht], T.D[0::16, :], T.ht[:])
-    d_pr = DMA("s", "dpr", [r_pts], T.D[2::16, :], T.pf1[:])
+    v_ha = V([v_pm], "ts", T.hA[:], T.pm[:], -16.0, 496.0, A.mult, A.add)
+    v_hb = V([v_pm], "ts", T.hB[:], T.pm[:], -16.0, 240.0, A.mult, A.add)
+    v_hta = V([v_ha, c_lta], "ts", T.htA[:], T.ltA[:], 0.0, T.hA[:], A.mult, A.add)
+    v_htb = V([v_hb, c_ltb], "ts", T.htB[:], T.ltB[:], 0.0, T.hB[:], A.mult, A.add)
+    v_pb = V([l_pts], "ts", T.pb[:], T.pti[:], 16.0, 16.0, A.mult, A.add)
+    v_pfb = V([], "ts", T.pfB[:], T.pti[:, 128:256], 16.0, 16.0, A.mult, A.add)
+    V([], "ms", T.WA[:, 0:2048], 0.0)
+    v_nls = V([l_nxt], "cp", T.nls[:], T.nxi[:])
+    v_ol = V([l_own], "cp", T.ol[:], T.owi[:])
+    v_wa = V([], "ms", T.WA[:, 2048:8192], 0.0)
+    DMA("s", "dda", [v_da, c_lta], T.DA[1::16, :], T.ltA[:])
+    DMA("s", "dda", [v_hta], T.DA[0::16, :], T.htA[:])
+    DMA("s", "ddb", [v_db, a2, c_ltb], T.DB[1::16, :], T.ltB[:])
+    DMA("s", "ddb", [v_htb], T.DB[0::16, :], T.htB[:])
+    d_a = DMA("s", "dda", [v_pb], T.DA[2::16, :], T.pb[:, 0:128])
+    d_b = DMA("s", "ddb", [v_pfb], T.DB[2::16, :], T.pfB[:])
+    DMA("s", "dprow", [], T.prow[:, 0:2048], T.pb[:, 0:128])
+    d_prow = DMA("s", "dprow", [], T.prow[:, 2048:4096], T.pb[:, 128:256])
 
-    IOTA([], T.WB[:, 6144:7168], [[0, 1024]], 0, 0)
-    p_z2 = IOTA([], T.WB[:, 7168:8192], [[0, 1024]], 0, 0)
-    v_wa = V([], "ms", T.WA[:], 0.0)
-    v_z = V([], "ms", T.BZ[:], 0.0)
-    V([], "ms", T.V2[:, 4096:4112], 0.0)
-    v_zx = V([], "ms", T.zx[:], 0.0)
-    v_nl = V([l_nxt], "cp", T.nl[:], T.nxi[:])
-    v_olb = V([r_own], "cp", T.ol[:, NA:256], T.own1[:, NA:256])
-    v_ola = V([], "cp", T.ol[:, 0:NA], T.own1[:, 0:NA])
-    v_pb = V([l_pts], "ts", T.pb[:], T.pti[:], 1.0, None, A.mult)
+    IOTA([], T.WB[:, 5632:6912], [[0, 1280]], 0, 0)
+    p_z2 = IOTA([], T.WB[:, 6912:8192], [[0, 1280]], 0, 0)
+    r_n = SEND([v_nls], nxc, T.nl[:], T.nls[:], "rn")
+    p_z = IOTA([], T.BZ[:], [[0, 704]], 0, 0)
 
-    s_b = ACT([a5, p_z2, v_olb, d_lh, d_pr], T.WB[:].indirect(T.ol[:, NA:256]), el(T.D, NA, 256), F.Silu)
-    s_a = V([v_wa, v_ola, d_lh, d_pr], "cp", T.WA[:].indirect(T.ol[:, 0:NA]), el(T.D, 0, NA))
-    d_prow = DMA("s", "dprow", [v_pb], T.prow[:], T.pb[:])
+    s_b = ACT([a5, p_z2, v_ol, d_b], T.WB[:].indirect(T.ol[:, 128:256]), T.DB[:], F.Silu)
+    s_a = V([v_wa, v_ol, d_a], "cp", T.WA[:].indirect(T.ol[:, 0:128]), T.DA[:])
+    v_one = V([], "ms", T.BO[:], 1.0)
+    v_neg = V([], "ms", T.NL[:], -1.0)
 
     BI, B2, B0, B8 = ((T.BZ, 144 * k) for k in range(4))
     ID = T.BZ[:, 576:704]
     E = (T.BO, 0)
     LS = T.BO[:, 144:272]
     SG = T.BO[:, 272:400]
+    GRP = [[-16, 8], [0, 16]]
+    PRG = [[16, 8], [0, 16]]
 
     def rowsel(mat, fills):
         buf = mat[0][:, mat[1]:mat[1] + 144]
-        tok = v_z
+        tok = p_z
         for k, w in fills:
             tok = SEL([tok], buf, [[-16, 9], [0, 16]], A.not_equal, w, -k, 1)
         return SEL([tok], buf, [[0, 9], [1, 16]], A.is_equal, 0.0, -15, 0)
 
-    m_bi = rowsel(BI, [(0, 16.0), (1, 0.0625)])
+    m_bi = rowsel(BI, [(0, 8.0), (1, 0.0625)])
+    m_b8 = SEL([p_z], T.BZ[:, 432:576], [[-1, 144]], A.not_equal, 0.0625, 15, 16)
     m_b2 = rowsel(B2, [(2, 0.0625)])
-    m_b8 = SEL([v_z], T.BZ[:, 432:576], [[-1, 144]], A.not_equal, 1.0, 15, 16)
-    c_d3 = IOTA([], T.d3[:], [[16, 16], [256, 16]], 0, 0)
-    c_ci = IOTA([], T.ci[:], [[1, 16]], 1025, 0)
-    c_mc = IOTA([], T.mc0[:], [[1, 64]], 0, 0)
-    m_id = SEL([v_z], ID, [[-1, 128]], A.not_equal, 1.0, 0, 1)
+    IOTA([], T.R[:, 4096:4112], [[0, 16]], 0, 0)
+    IOTA([], T.V2[:, 4096:4112], [[0, 16]], 0, 0)
+    v_zx = IOTA([], T.zx[:], [[0, 32]], 0, 0)
+    m_id = SEL([p_z], ID, [[-1, 128]], A.not_equal, 1.0, 0, 1)
 
-    t_pts = MM([m_b8, d_prow], rewrap(T.b7[:, 0:256], B8, T.prow, 0, 256, 8))
+    MM([m_b8, d_prow], rewrap(T.b7[:, 0:256], B8, T.prow, 0, 256, 8, False), False)
 
-    g_a = [ACT([s_b, v_nl], el(T.bg, c0, c1), T.WB[:].indirect(T.nl[:, c0:c1]), F.Copy) for c0, c1 in SUBS]
+    def tlist(out, src, c0, c1):
+        return [(out[0:c1 - c0, t:128:16], src[:, 16 * c0 + t:16 * c1:16], T.BZ[:, 159:287:16], True, True)
+                for t in range(16)]
+
+    g_a = [ACT([s_b, r_n], el(T.bg, c0, c1), T.WB[:].indirect(T.nl[:, c0:c1]), F.Copy) for c0, c1 in SUBS]
     upto = {}
     t_code = [None] * 4
-    t_fp = [None] * 4
     v_jl = [None] * 4
 
     def jl(q):
         v_jl[q] = V([t_code[q]], "ts", T.jl[:, 64 * q:64 * q + 64], T["b%d" % q][:, 0:64], -1.0, 4096.0, A.mult, A.add)
 
-    def fp(q):
-        t_fp[q] = MM([upto[64 * q + 64], m_b2], rewrap(T.b6[:, 64 * q:64 * q + 64], B2, T.R, 64 * q, 64 * q + 64))
-
+    r_y, r_x = [], []
     for k, (c0, c1) in enumerate(SUBS):
-        upto[c1] = V([s_a, g_a[k], v_nl], "tt", el(T.R, c0, c1), T.WA[:].indirect(T.nl[:, c0:c1]), el(T.bg, c0, c1), A.add)
+        upto[c1] = V([s_a, g_a[k], r_n], "tt", el(T.R, c0, c1), T.WA[:].indirect(T.nl[:, c0:c1]), el(T.bg, c0, c1), A.add)
         for s0, s1 in SENDS:
             if s1 == c1:
-                SEND([upto[c1]], el(T.V2, s0, s1), el(T.R, s0, s1), "rv", mask)
+                r_v = SEND([upto[c1]], opp, el(T.V2, s0, s1), el(T.R, s0, s1), "rv")
         if c1 % 64 == 0:
             q = c1 // 64 - 1
             t_code[q] = MM([upto[c1], m_bi], rewrap(T["b%d" % q][:, 0:64], BI, T.R, 64 * q, 64 * q + 64))
             if q == 1:
-                fp(0)
-            if q >= 2:
-                jl(q - 2)
-    fp(1)
-    fp(2)
-    v_one = V([], "ms", T.BO[:], 1.0)
-    v_neg = V([], "ms", T.NL[:], -1.0)
-    v_o1 = V([l_own], "ts", T.o1[:], T.owi[:], 1.0, None, A.add)
-    v_cc = V([v_pm], "ts", T.ccol[:], T.pm[:], 16.0, None, A.mult)
-    v_mcol = V([], "ts", T.mcol[:], T.pm[:], 64.0, -0.75, A.mult, A.add)
-    jl(2)
+                MM([m_b2], tlist(T.b6[:, 0:128], T.R, 0, 128), False)
+        if c1 == 32:
+            m = SEL([v_one], T.BO[:, 0:144], [[-16, 9], [0, 16]], A.is_ge, 0.0, 0, 1)
+            m = SEL([m], T.BO[:, 0:144], [[16, 9], [0, 16]], A.is_ge, 0.0, 15, -1)
+            m_e = SEL([m], T.BO[:, 0:144], [[0, 9], [1, 16]], A.is_equal, 0.0, -15, 0)
+        if c1 == 96:
+            m = SEL([v_one], LS, GRP, A.is_ge, 0.0, 0, 1)
+        if c1 == 128:
+            jl(0)
+            r_y.append(SEND([v_jl[0]], nxc, T.jy[:, 0:64], T.jl[:, 0:64], "ry0"))
+            m_ls = SEL([m], LS, [[1, 128]], A.is_gt, 0.0, 0, -1)
+        if c1 == 160:
+            m = SEL([v_one], SG, GRP, A.is_ge, 0.0, 0, 1)
+        if c1 == 192:
+            jl(1)
+            r_y.append(SEND([v_jl[1]], nxc, T.jy[:, 64:NY], T.jl[:, 64:NY], "ry1"))
+            m_sg = SEL([m], SG, PRG, A.is_ge, 0.0, 15, -1)
+        if c1 == 240:
+            jl(2)
+            r_x.append(SEND([v_jl[2]], prv, T.jx[:, 0:192 - NY], T.jl[:, NY:192], "rx0"))
+    m = SEL([v_neg], T.NL[:], PRG, A.is_ge, 0.0, 15, -1)
+    m = SEL([m], T.NL[:], [[-1, 128]], A.is_gt, 0.0, 0, 1)
+
+    gy2 = []
+    for r, (c0, cm, c1) in zip(r_y, ((0, 32, 64), (64, 80, NY))):
+        gy2.append(V([upto[256], r, v_zx], "cp", el(T.R2y, c0, cm), T.R[:].indirect(T.jy[:, c0:cm])))
+        gy2.append(ACT([upto[256], r, v_zx], el(T.R2y, cm, c1), T.R[:].indirect(T.jy[:, cm:c1]), F.Copy))
+        if c0 == 0:
+            v_kys = V([], "ms", T.kYs[96:128, :], 0.0)
+            v_o1 = V([l_own], "ts", T.o1[:], T.owi[:], 1.0, None, A.add)
+    jl(3)
+    r_x.append(SEND([v_jl[3]], prv, T.jx[:, 192 - NY:256 - NY], T.jl[:, 192:256], "rx1"))
+    m_nl = SEL([m], T.NL[:], [[-1, 128]], A.not_equal, 0.5, 0, 1)
+    c_ci = IOTA([], T.ci[:], [[1, 16]], 1025, 0)
+    c_mc = IOTA([], T.mc0[:], [[1, 64]], 0, 0)
+    t_ky = MM(gy2 + [v_jl[0], m_b2], tlist(T.b0, T.R2y, 0, NY))
+    a_ky = ACT([t_ky, v_zx], T.kYs[0:NY, :], T.b0[0:NY, 0:128], F.Copy)
+    r_k = SEND([a_ky, v_kys], opp, T.kYl[:], T.kYs[:], "rk")
+    t_kf = MM([], tlist(T.b6[:, 128:256], T.R, 128, 256))
+    m_b0 = rowsel(B0, [(0, 0.0625)])
+    c_d3 = IOTA([], T.d3[:], [[16, 16], [256, 16]], 0, 0)
+
     v_x1 = V([v_o1], "ts", T.x1[:], T.o1[:], 1, None, A.arith_shift_right)
     v_par = V([v_o1], "ts", T.par[:], T.o1[:], 1, None, A.bitwise_and)
     v_xw = V([v_x1], "ts", T.XW[:], T.x1[:], 2.0, -4096.0, A.mult, A.add)
-    v_pc = V([v_par], "ts", T.parc[:], T.par[:], 1024.0, -2.0, A.mult, A.add)
-    jl(3)
-    c_mk = V([], "ms", T.mk[:, 0:1024], 0.0)
-    c_ones = V([], "ms", T.ones[:], 1.0)
+    v_pb2 = V([v_par], "ts", T.parb[:], T.par[:], 1024.0, None, A.mult)
+    v_mcol = V([], "ts", T.mcol[:], T.pm[:], 64.0, -0.75, A.mult, A.add)
+
+    def gx(c0, c1):
+        return el(T.R2x, c0 - NY, c1 - NY), T.V2[:].indirect(T.jx[:, c0 - NY:c1 - NY])
+
+    g1 = [V([r_v, r_x[0], v_zx], "cp", *gx(96, 148)), ACT([r_v, r_x[0], v_zx], *gx(148, 192), F.Copy)]
+    a_kf = ACT([t_kf], T.kfs[:], T.b6[:, 0:256], F.Copy)
+    r_f = SEND([a_kf], prv, T.kfl[:], T.kfs[:], "rf")
+    c_mi = IOTA([], T.mi[:], [[1, 1024]], 0, 0)
+    g1 += [V([r_x[1]], "cp", *gx(192, 208)), ACT([r_x[1]], *gx(208, 224), F.Copy)]
+    g3 = [V([], "cp", *gx(224, 240)), ACT([], *gx(240, 256), F.Copy)]
+    c_mk = ACT([], T.mk[:, 0:1024], T.V2[:, 0:1024], F.Copy, None, 0.0)
+
+    def back(bank, c0, c1, kt):
+        n = c1 - c0
+        return [(bank[:, 0:n], kt[0:n, :], ID[0:n, 0:n], True, True)]
+
+    def into7(c0, c1, kt):
+        n = c1 - c0
+        return [(T.b7[:, c0:c1], kt[0:n, :], ID[0:n, 0:n], False, False)]
+
+    def kept(bank, c0, c1, tok):
+        return V([tok], "ts", T.kept[:, c0:c1], bank[:, 0:c1 - c0], 0.5, None, A.is_gt)
+
+    def zsum(s0, s1, first, last):
+        return [(T.b4[:, 0:16], moved(E, s), T.kept[:, 16 * s:16 * s + 16], first and s == s0, last and s == s1 - 1)
+                for s in range(s0, s1)]
+
+    t_k1 = MM(g1 + [v_jl[1]], tlist(T.b1, T.R2x, 0, 128))
+    t_by = MM([r_k, v_jl[3], m_id], back(T.b3, 0, NY, T.kYl))
+    t_k2 = MM(g3 + [v_jl[2]], tlist(T.b2, T.R2x, 128, 160))
+    V([], "ms", T.ones[:], 1.0)
+    v_cc = V([v_pm], "ts", T.ccol[:], T.pm[:], 16.0, None, A.mult)
     v_cst = V([v_cc, c_ci], "ts", T.cst[:], T.ci[:], T.ccol[:], None, A.add)
     v_mc = V([v_mcol, c_mc], "ts", T.mcs[:], T.mc0[:], T.mcol[:], None, A.add)
-
-    GRP = [[-16, 8], [0, 16]]
-    PRG = [[16, 8], [0, 16]]
-    m = SEL([v_one], T.BO[:, 0:144], [[-16, 9], [0, 16]], A.is_ge, 0.0, 0, 1)
-    m = SEL([m], T.BO[:, 0:144], [[16, 9], [0, 16]], A.is_ge, 0.0, 15, -1)
-    m_e = SEL([m], T.BO[:, 0:144], [[0, 9], [1, 16]], A.is_equal, 0.0, -15, 0)
-    m = SEL([v_one], LS, GRP, A.is_ge, 0.0, 0, 1)
-    m_ls = SEL([m], LS, [[1, 128]], A.is_gt, 0.0, 0, -1)
-    m = SEL([v_one], SG, GRP, A.is_ge, 0.0, 0, 1)
-    m_sg = SEL([m], SG, PRG, A.is_ge, 0.0, 15, -1)
-    m = SEL([v_neg], T.NL[:], PRG, A.is_ge, 0.0, 15, -1)
-    m = SEL([m], T.NL[:], [[-1, 128]], A.is_gt, 0.0, 0, 1)
-    m_nl = SEL([m], T.NL[:], [[-1, 128]], A.not_equal, 0.5, 0, 1)
-    m_b0 = rowsel(B0, [(0, 0.0625)])
-    c_mi = IOTA([], T.mi[:], [[1, 1024]], 0, 0)
-
-    r_v = ("rv", len(SENDS) * len(eng))
-    g2 = []
-    for q in range(4):
-        c0, cm, c1 = 64 * q, 64 * q + 32, 64 * q + 64
-        g2.append(V([r_v, v_jl[q], v_zx], "cp", el(T.R2, c0, cm), T.V2[:].indirect(T.jl[:, c0:cm])))
-        g2.append(ACT([r_v, v_jl[q], v_zx], el(T.R2, cm, c1), T.V2[:].indirect(T.jl[:, cm:c1]), F.Copy))
-
-    def kt(h):
-        return [(T["b%d" % h][:, t:128:16], T.R2[:, 2048 * h + t:2048 * h + 2048:16], T.BZ[:, 159:287:16], True, True)
-                for t in range(16)]
-
-    def evac(h, tok):
-        return V([tok], "cp", T.kT[:, 128 * h:128 * h + 128], T["b%d" % h][:, 0:128])
-
-    def back(h, tok):
-        return MM([tok, m_id], [(T["b%d" % (2 + h)][:, 0:128], T.kT[:, 128 * h:128 * h + 128], ID, True, True)])
-
-    def kept(h, tok):
-        return V([tok], "ts", T.kept[:, 128 * h:128 * h + 128], T["b%d" % (2 + h)][:, 0:128], 0.5, None, A.is_gt)
-
-    def zsum(s0, s1):
-        return [(T.b4[:, 0:16], moved(E, s), T.kept[:, 16 * s:16 * s + 16], s == 0, s == 15) for s in range(s0, s1)]
-
-    t_kt0 = MM(g2[:4] + [m_b2] + v_jl, kt(0))
-    v_t0 = evac(0, t_kt0)
-    kt1 = kt(1)
-    MM(g2[4:], kt1[:8], False)
-    t_k0 = back(0, v_t0)
-    t_kt1 = MM([], kt1[8:])
-    v_k0 = kept(0, t_k0)
-    v_t1 = evac(1, t_kt1)
-    MM([v_k0, m_e], zsum(0, 4), False)
-    t_k1 = back(1, v_t1)
-    MM([], zsum(4, 8), False)
-    v_k1 = kept(1, t_k1)
-    t_z = MM([v_k1], zsum(8, 16))
-    t_k2 = [t_k0, t_k1]
-    v_b0 = V([v_pc, t_pts], "tt", T.base0[:], T.b7[:, 0:256], T.parc[:], A.add)
+    v_k1 = V([t_k1], "cp", T.kX1[:], T.b1[:, 0:128])
+    v_cy = kept(T.b3, 0, NY, t_by)
+    t_b1 = MM([v_k1, a_ky], back(T.b0, 96, 224, T.kX1))
+    MM([v_cy, m_e], zsum(0, 4, True, False), False)
+    v_k2 = V([t_k2], "cp", T.kX2[:], T.b2[0:32, 0:128])
+    v_c1 = kept(T.b0, 96, 224, t_b1)
+    t_b2 = MM([v_k2], back(T.b1, 224, 256, T.kX2))
+    v_c2 = kept(T.b1, 224, 256, t_b2)
     v_e16 = V([m_e], "cp", T.E16[:], T.BO[:, 0:144])
     V([m_id], "cp", T.I16[:], ID)
     v_i4k = V([], "ts", T.I4k[:], ID, 4096.0, None, A.mult)
-    v_zc = V([t_z, c_ones, v_zx], "scan", T.zx[:, 1:17], T.ones[:, 0:16], T.b4[:, 0:16], 0.0, A.mult, A.add)
+    MM([], zsum(4, 6, False, False), False)
+    MM([v_c1], zsum(6, 14, False, False), False)
+    t_z = MM([v_c2], zsum(14, 16, False, True))
+    v_zc = V([t_z, v_pb2, v_zx], "scan", T.zx[:, 1:17], T.ones[:, 0:16], T.b4[:, 0:16], 0.0, A.mult, A.add)
     t_off = MM([v_zc, m_ls], [(T.b5[:, 0:1], LS, T.zx[:, 16:17], True, True)])
     v_e0 = V([t_z], "ts", T.e0[:], T.b4[:, 0:16], 0.0, None, A.is_equal)
     v_e1 = V([v_e0, v_cst], "tt", T.e1[:], T.e0[:], T.cst[:], A.mult)
     v_p1 = V([v_e1, v_zc], "tt", T.p1[:], T.e1[:], T.zx[:, 0:16], A.add)
     v_zl = V([v_p1, t_off], "ts", T.zl[:], T.p1[:], T.b5[:, 0:1], None, A.add)
-    MM([m_sg, v_b0], [(T.b7[:, 0:256], SG, T.kept[:], True, True)])
-    t_n1 = MM([m_nl], [(T.b7[:, 256:512], T.NL[:], T.kept[:], True, True)])
-    fp(3)
+    MM([m_sg], [(T.b3[:, 0:256], SG, T.kept[:], True, True)], False)
+    t_n1 = MM([m_nl], [(T.b3[:, 256:512], T.NL[:], T.kept[:], True, True)])
+    MM([], into7(96, 224, T.kX1) + into7(0, NY, T.kYl) + into7(224, 256, T.kX2), False)
+    MM([r_f], into7(0, 128, T.kfl[:, 0:128]) + into7(128, 256, T.kfl[:, 128:256]), False)
+    t_y7 = MM([v_pb2], [(T.b7[:, 0:256], ID, T.parb[:], False, True)])
+    a_yw = ACT([t_y7], T.YW[:], T.b7[:, 0:256], F.Identity, -3.0)
     v_mks = V([v_zl, c_mk, c_d3], "cp", T.mk[:].indirect(T.zl[:]), T.d3[:])
     v_blk = V([v_mks], "scan", T.blk[:], T.mk[:, 0:1024], T.mk[:, 0:1024], 0.0, A.max, A.max)
     t_bl = MM([v_blk, m_b0, v_zl], rewrap(T.b5[:, 64:128], B0, T.blk, 0, 64))
-    v_cum = V([t_n1], "scan", T.cum[:], T.ones[:], T.b7[:, 0:256], -1.5, A.mult, A.add)
-    v_base = V([v_b0, t_fp[3]], "tt", T.base[:], T.b6[:, 0:256], T.base0[:], A.add)
-    v_kw = V([v_cum], "tt", T.KW[:], T.b7[:, 256:512], T.cum[:], A.add)
-    v_yw = None
-    for h in range(2):
-        c0, c1 = 128 * h, 128 * h + 128
-        v_yw = V([t_k2[h], v_base], "tt", T.YW[:, c0:c1], T["b%d" % (2 + h)][:, 0:128], T.base[:, c0:c1], A.add)
+    v_cum = V([t_n1], "scan", T.cum[:], T.ones[:], T.b3[:, 0:256], -1.5, A.mult, A.add)
+    v_kw = V([v_cum], "tt", T.KW[:], T.b3[:, 256:512], T.cum[:], A.add)
+    v_f = V([v_mc, v_cum], "ts", T.F4[:], T.mcs[:], T.cum[:, 255:256], 4096.0, A.is_le, A.mult)
     v_bl = V([t_bl], "cp", T.bl[:], T.b5[:, 64:128])
 
     def osum(dst, src, xs, first, last):
@@ -358,22 +395,26 @@ def rank_program(g, core, T, topo):
     PX, PY = T.b4[:, 64:128], T.b6[:, 256:320]
     bl = [T.bl[:, 0:32], T.bl[:, 32:64]]
     hs = [(0, 512), (512, 1024)]
-    a_gy = ACT([v_yw, v_bl], T.gy[:], T.YW[:].indirect(bl[0]), F.Copy)
+    a_gy = [ACT([a_yw, v_bl], T.gy[:, m0:m1], T.YW[:].indirect(T.bl[:, m0 // 16:m1 // 16]), F.Copy)
+            for m0, m1 in ((0, 512), (512, 640))]
     v_hit = [V([v_kw, v_bl, c_mi], "tt", T.hit[:, m0:m1], T.KW[:].indirect(bl[h]), T.mi[:, m0:m1], A.is_equal)
              for h, (m0, m1) in enumerate(hs)]
     v_hx = [V([v_hit[h], v_xw], "tt", T.hx[:, m0:m1], T.XW[:].indirect(bl[h]), T.hit[:, m0:m1], A.mult)
             for h, (m0, m1) in enumerate(hs)]
-    v_f = V([v_mc, v_cum], "ts", T.F4[:], T.mcs[:], T.cum[:, 255:256], 4096.0, A.is_le, A.mult)
-    v_hy = [V([v_hit[1], v_yw], "tt", T.hy[:, n:n + 256], T.YW[:].indirect(T.bl[:, n // 16:n // 16 + 16]), T.hit[:, n:n + 256],
-              A.mult) for n in (512, 768)]
-    MM([a_gy, v_i4k], [(T.b0[:], T.I16[:], T.gy[:], True, False)], False)
+    v_hy = [V([v_hit[1], a_yw], "tt", T.hy[:, n:n + 192], T.YW[:].indirect(T.bl[:, n // 16:n // 16 + 12]), T.hit[:, n:n + 192],
+              A.mult) for n in (640, 832)]
+    MM([a_gy[0], v_i4k], [(T.b0[:], T.I16[:], T.gy[:, 0:512], True, False)], False)
     t_m = MM([v_hit[0]], [(T.b0[:], T.I4k[:], T.hit[:, 0:512], False, True)])
+    MM([a_gy[1]], [(T.b1[:, 0:128], T.I16[:], T.gy[:, 512:640], True, False)], False)
+    t_m2 = MM([v_hit[1]], [(T.b1[:, 0:128], T.I4k[:], T.hit[:, 512:640], False, True)])
     a_hy = ACT([t_m], T.hy[:, 0:512], T.b0[:], F.Relu, -4096.0)
+    a_hy2 = ACT([t_m2], T.hy[:, 512:640], T.b1[:, 0:128], F.Relu, -4096.0)
     MM([v_hx[0], v_e16, v_zc, v_e1], osum(PX, T.hx, range(0, 8), True, False), False)
-    MM([a_hy, v_base], osum(PY, T.hy, range(0, 8), True, False), False)
+    MM([a_hy, a_kf], osum(PY, T.hy, range(0, 8), True, False), False)
+    MM([a_hy2], osum(PY, T.hy, range(8, 10), False, False), False)
     t_x = MM([v_hx[1]], osum(PX, T.hx, range(8, 16), False, True))
-    MM([v_hy[0]], osum(PY, T.hy, range(8, 12), False, False), False)
-    t_y = MM([v_hy[1]], osum(PY, T.hy, range(12, 16), False, True))
+    MM([v_hy[0]], osum(PY, T.hy, range(10, 13), False, False), False)
+    t_y = MM([v_hy[1]], osum(PY, T.hy, range(13, 16), False, True))
     v_ox = V([v_f, t_x], "tt", T.ox[:], PX, T.F4[:], A.add)
     v_pa = V([t_y], "ts", T.pa[:], PY, 1023.5, -1.0, A.is_ge, A.add)
     v_pm2 = V([], "ts", T.pc[:], PY, 1023.5, -1024.0, A.is_ge, A.mult)

@@ -14,8 +14,8 @@ SCRATCH = {
     "htB": ("sbuf", [128, 128], "float32"),
     "ol": ("sbuf", [128, 256], "uint16"),
     "jl": ("sbuf", [128, 256], "uint16"),
-    "jy": ("sbuf", [128, 96], "uint16"),
-    "jx": ("sbuf", [128, 160], "uint16"),
+    "jy": ("sbuf", [128, 128], "uint16"),
+    "jx": ("sbuf", [128, 128], "uint16"),
     "DA": ("sbuf", [128, 2048], "bfloat16"),
     "DB": ("sbuf", [128, 2048], "float32"),
     "WA": ("sbuf", [128, 8192], "bfloat16"),
@@ -23,39 +23,32 @@ SCRATCH = {
     "bg": ("sbuf", [128, 4096], "bfloat16"),
     "R": ("sbuf", [128, 4112], "bfloat16"),
     "V2": ("sbuf", [128, 4112], "bfloat16"),
-    "R2y": ("sbuf", [128, 1536], "bfloat16"),
-    "R2x": ("sbuf", [128, 2560], "bfloat16"),
+    "R2y": ("sbuf", [128, 2048], "bfloat16"),
+    "R2x": ("sbuf", [128, 2048], "bfloat16"),
     "prow": ("sbuf", [8, 4096], "bfloat16"),
     "pid": ("sbuf", [128, 1], "int32"),
     "pm": ("sbuf", [128, 1], "int32"),
     "hA": ("sbuf", [128, 1], "float32"),
     "hB": ("sbuf", [128, 1], "float32"),
     "ccol": ("sbuf", [128, 1], "float32"),
-    "mcol": ("sbuf", [128, 1], "float32"),
+    "padc": ("sbuf", [128, 1], "float32"),
     "ci": ("sbuf", [128, 16], "float32"),
     "cst": ("sbuf", [128, 16], "float32"),
-    "mc0": ("sbuf", [128, 64], "float32"),
-    "mcs": ("sbuf", [128, 64], "float32"),
     "BZ": ("sbuf", [128, 704], "bfloat16"),
     "BO": ("sbuf", [128, 400], "bfloat16"),
     "NL": ("sbuf", [128, 128], "bfloat16"),
-    "E16": ("sbuf", [128, 144], "float16"),
-    "I16": ("sbuf", [128, 128], "float16"),
-    "I4k": ("sbuf", [128, 128], "float16"),
+    "E4": ("sbuf", [128, 144], "bfloat16"),
     "ones": ("sbuf", [128, 256], "float32"),
     "d3": ("sbuf", [128, 256], "bfloat16"),
-    "mi": ("sbuf", [128, 1024], "float32"),
+    "mi": ("sbuf", [128, 512], "float32"),
     "mk": ("sbuf", [128, 2320], "bfloat16"),
     "blk": ("sbuf", [128, 1024], "bfloat16"),
     "bl": ("sbuf", [128, 64], "uint16"),
-    "o1": ("sbuf", [128, 256], "int32"),
-    "x1": ("sbuf", [128, 256], "int32"),
-    "par": ("sbuf", [128, 256], "int32"),
-    "parb": ("sbuf", [128, 256], "bfloat16"),
+    "blc": ("sbuf", [128, 64], "bfloat16"),
+    "off": ("sbuf", [128, 64], "uint16"),
     "kYs": ("sbuf", [128, 128], "bfloat16"),
     "kYl": ("sbuf", [128, 128], "bfloat16"),
     "kX1": ("sbuf", [128, 128], "bfloat16"),
-    "kX2": ("sbuf", [32, 128], "bfloat16"),
     "kfs": ("sbuf", [128, 256], "bfloat16"),
     "kfl": ("sbuf", [128, 256], "bfloat16"),
     "kept": ("sbuf", [128, 256], "bfloat16"),
@@ -66,27 +59,20 @@ SCRATCH = {
     "zl": ("sbuf", [128, 16], "uint16"),
     "cum": ("sbuf", [128, 256], "float32"),
     "KW": ("sbuf", [128, 256], "float32"),
-    "XW": ("sbuf", [128, 256], "float32"),
+    "KV": ("sbuf", [128, 256], "float32"),
     "YW": ("sbuf", [128, 256], "float32"),
-    "gy": ("sbuf", [128, 640], "float16"),
-    "hit": ("sbuf", [128, 1024], "float16"),
-    "hx": ("sbuf", [128, 1024], "float16"),
-    "hy": ("sbuf", [128, 1024], "float16"),
-    "F4": ("sbuf", [128, 64], "float32"),
-    "ox": ("sbuf", [128, 64], "float32"),
-    "pa": ("sbuf", [128, 64], "float32"),
-    "pc": ("sbuf", [128, 64], "float32"),
-    "ok": ("sbuf", [128, 64], "float32"),
-    "osum": ("sbuf", [128, 64], "float32"),
+    "owf": ("sbuf", [128, 256], "float32"),
+    "hit": ("sbuf", [128, 1024], "bfloat16"),
+    "res": ("sbuf", [128, 1024], "float32"),
 }
 for _k in range(8):
     SCRATCH["b%d" % _k] = ("psum", [128, 512], "float32")
-SEMAPHORES = ["v", "a", "t", "p", "down", "dpts", "dnxt", "dda", "ddb", "dprow", "dout",
+SEMAPHORES = ["v", "a", "t", "p", "down", "dptb", "dpts", "dnxt", "dda", "ddb", "dprow", "dwin", "dout",
               "rn", "rv", "ry0", "ry1", "rx0", "rx1", "rk", "rf", "sent"]
 
 SUBS = [(0, 16), (16, 32)] + [(k, k + 32) for k in range(32, 224, 32)] + [(224, 240), (240, 256)]
 SENDS = [(0, 32), (32, 96), (96, 160), (160, 224), (224, 256)]
-NY = 96
+NY = 128
 
 
 def rank_program(g, core, T, topo):
@@ -147,6 +133,10 @@ def rank_program(g, core, T, topo):
         need("p", toks)
         return done("p", g.affine_select(buf, buf, pattern, cmp, fill, base, cm), 1)
 
+    def SELO(toks, out, src, pattern, cmp, base, cm):
+        need("p", toks)
+        return done("p", g.affine_select(out, src, pattern, cmp, 0.0, base, cm), 1)
+
     def DMA(q, s, toks, out, in_):
         need(q, toks)
         return done(s, queues[q].dma_start(out, in_), 16)
@@ -172,15 +162,16 @@ def rank_program(g, core, T, topo):
         buf, c = mat
         return buf[0:K, c + 15 - t:c + 143 - t]
 
-    def rewrap(out, mat, src, c0, c1, K=128, close=True):
-        return [(out, moved(mat, t, K), src[0:K, 16 * c0 + t:16 * c1:16], t == 0, close and t == 15) for t in range(16)]
+    def rewrap(out, mat, src, c0, c1, K=128, close=True, first=True):
+        return [(out, moved(mat, t, K), src[0:K, 16 * c0 + t:16 * c1:16], first and t == 0, close and t == 15)
+                for t in range(16)]
 
     def el(buf, c0, c1):
         return buf[:, 16 * c0:16 * c1]
 
     l_own = DMA("s", "down", [], T.owi[:], T.own[:])
-    DMA("a", "dpts", [], T.pti[:, 0:128], T.pts[:, 0:2048])
-    l_pts = DMA("a", "dpts", [], T.pti[:, 128:256], T.pts[:, 2048:4096])
+    l_ptb = DMA("a", "dptb", [], T.pti[:, 128:256], T.pts[:, 2048:4096])
+    l_pts = DMA("a", "dpts", [], T.pti[:, 0:128], T.pts[:, 0:2048])
     l_nxt = DMA("s", "dnxt", [], T.nxi[:], T.nxt[:])
 
     c_pid = IOTA([], T.pid[:], [[1, 1]], 0, 1, False)
@@ -189,50 +180,48 @@ def rank_program(g, core, T, topo):
     z0 = V([], "ms", T.WB[:, 0:128], 0.0)
     v_da = V([], "ms", T.DA[:], 0.0)
     z1 = V([], "ms", T.WB[:, 256:1024], 0.0)
-    v_db = V([], "ms", T.DB[:, 0:768], 0.0)
-    a1 = ACT([z0], T.WB[:, 128:256], T.WB[:, 0:128], F.Silu)
-    ACT([a1, z1], T.DB[:, 768:1792], T.WB[:, 0:1024], F.Silu)
-    a2 = ACT([], T.DB[:, 1792:2048], T.WB[:, 0:256], F.Silu)
-    a3 = ACT([], T.WB[:, 1024:2048], T.WB[:, 0:1024], F.Silu)
-    ACT([a3], T.WB[:, 2048:4096], T.WB[:, 0:2048], F.Silu)
-    a5 = ACT([a3], T.WB[:, 4096:5632], T.WB[:, 0:1536], F.Silu)
+    v_db = V([], "ms", T.DB[:, 0:640], 0.0)
     v_pm = V([c_pid], "ts", T.pm[:], T.pid[:], 15, None, A.bitwise_and)
     v_ha = V([v_pm], "ts", T.hA[:], T.pm[:], -16.0, 496.0, A.mult, A.add)
     v_hb = V([v_pm], "ts", T.hB[:], T.pm[:], -16.0, 240.0, A.mult, A.add)
-    v_hta = V([v_ha, c_lta], "ts", T.htA[:], T.ltA[:], 0.0, T.hA[:], A.mult, A.add)
-    v_htb = V([v_hb, c_ltb], "ts", T.htB[:], T.ltB[:], 0.0, T.hB[:], A.mult, A.add)
-    v_pb = V([l_pts], "ts", T.pb[:], T.pti[:], 16.0, 16.0, A.mult, A.add)
-    v_pfb = V([], "ts", T.pfB[:], T.pti[:, 128:256], 16.0, 16.0, A.mult, A.add)
+    a1 = ACT([z0], T.WB[:, 128:256], T.WB[:, 0:128], F.Silu)
+    ACT([a1, z1], T.DB[:, 640:1664], T.WB[:, 0:1024], F.Silu)
+    a2 = ACT([], T.DB[:, 1664:2048], T.WB[:, 0:384], F.Silu)
+    a_htb = ACT([v_hb], T.htB[:], T.WB[:, 0:128], F.Identity, T.hB[:])
+    a_hta = ACT([v_ha], T.htA[:], T.WB[:, 0:128], F.Identity, T.hA[:])
+    a3 = ACT([], T.WB[:, 1024:2048], T.WB[:, 0:1024], F.Silu)
+    ACT([a3], T.WB[:, 2048:4096], T.WB[:, 0:2048], F.Silu)
+    a5 = ACT([a3], T.WB[:, 4096:5248], T.WB[:, 0:1152], F.Silu)
+    v_pfb = V([l_ptb], "ts", T.pfB[:], T.pti[:, 128:256], 16.0, 16.0, A.mult, A.add)
     V([], "ms", T.WA[:, 0:2048], 0.0)
-    v_nls = V([l_nxt], "cp", T.nls[:], T.nxi[:])
     v_ol = V([l_own], "cp", T.ol[:], T.owi[:])
-    v_wa = V([], "ms", T.WA[:, 2048:8192], 0.0)
+    v_pb = V([l_pts], "ts", T.pb[:], T.pti[:], 16.0, 16.0, A.mult, A.add)
+    V([], "ms", T.WA[:, 2048:5120], 0.0)
+    v_nls = V([l_nxt], "cp", T.nls[:], T.nxi[:])
+    v_wa = V([], "ms", T.WA[:, 5120:8192], 0.0)
     DMA("s", "dda", [v_da, c_lta], T.DA[1::16, :], T.ltA[:])
-    DMA("s", "dda", [v_hta], T.DA[0::16, :], T.htA[:])
     DMA("s", "ddb", [v_db, a2, c_ltb], T.DB[1::16, :], T.ltB[:])
-    DMA("s", "ddb", [v_htb], T.DB[0::16, :], T.htB[:])
+    DMA("s", "ddb", [v_pfb], T.DB[2::16, :], T.pfB[:])
+    d_b = DMA("s", "ddb", [a_htb], T.DB[0::16, :], T.htB[:])
+    DMA("s", "dda", [a_hta], T.DA[0::16, :], T.htA[:])
     d_a = DMA("s", "dda", [v_pb], T.DA[2::16, :], T.pb[:, 0:128])
-    d_b = DMA("s", "ddb", [v_pfb], T.DB[2::16, :], T.pfB[:])
     DMA("s", "dprow", [], T.prow[:, 0:2048], T.pb[:, 0:128])
     d_prow = DMA("s", "dprow", [], T.prow[:, 2048:4096], T.pb[:, 128:256])
 
-    IOTA([], T.WB[:, 5632:6912], [[0, 1280]], 0, 0)
-    p_z2 = IOTA([], T.WB[:, 6912:8192], [[0, 1280]], 0, 0)
+    IOTA([], T.WB[:, 5248:6720], [[0, 1472]], 0, 0)
+    p_z2 = IOTA([], T.WB[:, 6720:8192], [[0, 1472]], 0, 0)
     r_n = SEND([v_nls], nxc, T.nl[:], T.nls[:], "rn")
     p_z = IOTA([], T.BZ[:], [[0, 704]], 0, 0)
 
     s_b = ACT([a5, p_z2, v_ol, d_b], T.WB[:].indirect(T.ol[:, 128:256]), T.DB[:], F.Silu)
     s_a = V([v_wa, v_ol, d_a], "cp", T.WA[:].indirect(T.ol[:, 0:128]), T.DA[:])
-    v_one = V([], "ms", T.BO[:], 1.0)
-    v_neg = V([], "ms", T.NL[:], -1.0)
 
     BI, B2, B0, B8 = ((T.BZ, 144 * k) for k in range(4))
     ID = T.BZ[:, 576:704]
     E = (T.BO, 0)
+    E256 = (T.E4, 0)
     LS = T.BO[:, 144:272]
     SG = T.BO[:, 272:400]
-    GRP = [[-16, 8], [0, 16]]
-    PRG = [[16, 8], [0, 16]]
 
     def rowsel(mat, fills):
         buf = mat[0][:, mat[1]:mat[1] + 144]
@@ -248,8 +237,11 @@ def rank_program(g, core, T, topo):
     IOTA([], T.V2[:, 4096:4112], [[0, 16]], 0, 0)
     v_zx = IOTA([], T.zx[:], [[0, 32]], 0, 0)
     m_id = SEL([p_z], ID, [[-1, 128]], A.not_equal, 1.0, 0, 1)
+    IOTA([], T.BO[:, 128:144], [[0, 16]], 0, 0)
+    p_one = IOTA([], SG, [[0, 128]], 1, 0)
 
-    MM([m_b8, d_prow], rewrap(T.b7[:, 0:256], B8, T.prow, 0, 256, 8, False), False)
+    MM([m_b8, d_prow], rewrap(T.b7[:, 0:128], B8, T.prow, 0, 128, 8, False)
+       + rewrap(T.b5[:, 0:128], B8, T.prow, 128, 256, 8, False), False)
 
     def tlist(out, src, c0, c1):
         return [(out[0:c1 - c0, t:128:16], src[:, 16 * c0 + t:16 * c1:16], T.BZ[:, 159:287:16], True, True)
@@ -275,70 +267,56 @@ def rank_program(g, core, T, topo):
             if q == 1:
                 MM([m_b2], tlist(T.b6[:, 0:128], T.R, 0, 128), False)
         if c1 == 32:
-            m = SEL([v_one], T.BO[:, 0:144], [[-16, 9], [0, 16]], A.is_ge, 0.0, 0, 1)
-            m = SEL([m], T.BO[:, 0:144], [[16, 9], [0, 16]], A.is_ge, 0.0, 15, -1)
-            m_e = SEL([m], T.BO[:, 0:144], [[0, 9], [1, 16]], A.is_equal, 0.0, -15, 0)
+            m = SEL([p_one], SG, [[-16, 8], [0, 16]], A.is_ge, 0.0, 0, 1)
         if c1 == 96:
-            m = SEL([v_one], LS, GRP, A.is_ge, 0.0, 0, 1)
+            m_sg = SEL([m], SG, [[16, 8], [0, 16]], A.is_ge, 0.0, 15, -1)
         if c1 == 128:
             jl(0)
             r_y.append(SEND([v_jl[0]], nxc, T.jy[:, 0:64], T.jl[:, 0:64], "ry0"))
-            m_ls = SEL([m], LS, [[1, 128]], A.is_gt, 0.0, 0, -1)
         if c1 == 160:
-            m = SEL([v_one], SG, GRP, A.is_ge, 0.0, 0, 1)
+            m_e = SELO([m_sg], T.BO[:, 0:128], SG, [[0, 8], [1, 16]], A.is_equal, -15, 0)
         if c1 == 192:
             jl(1)
             r_y.append(SEND([v_jl[1]], nxc, T.jy[:, 64:NY], T.jl[:, 64:NY], "ry1"))
-            m_sg = SEL([m], SG, PRG, A.is_ge, 0.0, 15, -1)
         if c1 == 240:
             jl(2)
             r_x.append(SEND([v_jl[2]], prv, T.jx[:, 0:192 - NY], T.jl[:, NY:192], "rx0"))
-    m = SEL([v_neg], T.NL[:], PRG, A.is_ge, 0.0, 15, -1)
-    m = SEL([m], T.NL[:], [[-1, 128]], A.is_gt, 0.0, 0, 1)
 
     gy2 = []
-    for r, (c0, cm, c1) in zip(r_y, ((0, 32, 64), (64, 80, NY))):
+    for r, (c0, cm, c1) in zip(r_y, ((0, 32, 64), (64, 96, NY))):
         gy2.append(V([upto[256], r, v_zx], "cp", el(T.R2y, c0, cm), T.R[:].indirect(T.jy[:, c0:cm])))
         gy2.append(ACT([upto[256], r, v_zx], el(T.R2y, cm, c1), T.R[:].indirect(T.jy[:, cm:c1]), F.Copy))
         if c0 == 0:
-            v_kys = V([], "ms", T.kYs[96:128, :], 0.0)
-            v_o1 = V([l_own], "ts", T.o1[:], T.owi[:], 1.0, None, A.add)
-    jl(3)
-    r_x.append(SEND([v_jl[3]], prv, T.jx[:, 192 - NY:256 - NY], T.jl[:, 192:256], "rx1"))
-    m_nl = SEL([m], T.NL[:], [[-1, 128]], A.not_equal, 0.5, 0, 1)
+            v_owf = V([l_own], "cp", T.owf[:], T.owi[:])
+            jl(3)
+            r_x.append(SEND([v_jl[3]], prv, T.jx[:, 192 - NY:256 - NY], T.jl[:, 192:256], "rx1"))
     c_ci = IOTA([], T.ci[:], [[1, 16]], 1025, 0)
-    c_mc = IOTA([], T.mc0[:], [[1, 64]], 0, 0)
-    t_ky = MM(gy2 + [v_jl[0], m_b2], tlist(T.b0, T.R2y, 0, NY))
-    a_ky = ACT([t_ky, v_zx], T.kYs[0:NY, :], T.b0[0:NY, 0:128], F.Copy)
-    r_k = SEND([a_ky, v_kys], opp, T.kYl[:], T.kYs[:], "rk")
-    t_kf = MM([], tlist(T.b6[:, 128:256], T.R, 128, 256))
-    m_b0 = rowsel(B0, [(0, 0.0625)])
+    t_kf = MM([m_b2], tlist(T.b6[:, 128:256], T.R, 128, 256))
+    a_kf = ACT([t_kf], T.kfs[:], T.b6[:, 0:256], F.Copy)
+    r_f = SEND([a_kf], prv, T.kfl[:], T.kfs[:], "rf")
+    t_ky = MM(gy2 + [v_jl[0]], tlist(T.b0, T.R2y, 0, NY))
+    a_ky = ACT([t_ky], T.kYs[:], T.b0[:, 0:128], F.Copy)
+    r_k = SEND([a_ky], opp, T.kYl[:], T.kYs[:], "rk")
+    p_ones = IOTA([], T.ones[:], [[0, 256]], 1, 0)
     c_d3 = IOTA([], T.d3[:], [[16, 16], [256, 16]], 0, 0)
-
-    v_x1 = V([v_o1], "ts", T.x1[:], T.o1[:], 1, None, A.arith_shift_right)
-    v_par = V([v_o1], "ts", T.par[:], T.o1[:], 1, None, A.bitwise_and)
-    v_xw = V([v_x1], "ts", T.XW[:], T.x1[:], 2.0, -4096.0, A.mult, A.add)
-    v_pb2 = V([v_par], "ts", T.parb[:], T.par[:], 1024.0, None, A.mult)
-    v_mcol = V([], "ts", T.mcol[:], T.pm[:], 64.0, -0.75, A.mult, A.add)
+    m_ls = SELO([m_sg], LS, SG, [[1, 128]], A.is_gt, 0, -1)
+    m_nl = SELO([m_sg], T.NL[:], SG, [[-1, 128]], A.is_gt, 0, 1)
+    m_b0 = rowsel(B0, [(0, 0.0625)])
+    c_mi = IOTA([], T.mi[:], [[1, 512]], 0, 0)
 
     def gx(c0, c1):
         return el(T.R2x, c0 - NY, c1 - NY), T.V2[:].indirect(T.jx[:, c0 - NY:c1 - NY])
 
-    g1 = [V([r_v, r_x[0], v_zx], "cp", *gx(96, 148)), ACT([r_v, r_x[0], v_zx], *gx(148, 192), F.Copy)]
-    a_kf = ACT([t_kf], T.kfs[:], T.b6[:, 0:256], F.Copy)
-    r_f = SEND([a_kf], prv, T.kfl[:], T.kfs[:], "rf")
-    c_mi = IOTA([], T.mi[:], [[1, 1024]], 0, 0)
-    g1 += [V([r_x[1]], "cp", *gx(192, 208)), ACT([r_x[1]], *gx(208, 224), F.Copy)]
-    g3 = [V([], "cp", *gx(224, 240)), ACT([], *gx(240, 256), F.Copy)]
-    c_mk = ACT([], T.mk[:, 0:1024], T.V2[:, 0:1024], F.Copy, None, 0.0)
+    g1 = [V([r_v, r_x[0], v_zx], "cp", *gx(128, 164)), ACT([r_v, r_x[0], v_zx], *gx(164, 192), F.Copy)]
+    g2 = [V([r_x[1]], "cp", *gx(192, 224)), ACT([r_x[1]], *gx(224, 256), F.Copy)]
+    DMA("s", "dwin", [v_owf, g_a[-1], g2[1]], T.WB[0::16, 0:4096], T.owf[:])
 
     def back(bank, c0, c1, kt):
         n = c1 - c0
         return [(bank[:, 0:n], kt[0:n, :], ID[0:n, 0:n], True, True)]
 
-    def into7(c0, c1, kt):
-        n = c1 - c0
-        return [(T.b7[:, c0:c1], kt[0:n, :], ID[0:n, 0:n], False, False)]
+    def plus(bank, kt, last):
+        return [(bank[:, 0:128], kt, ID, False, last)]
 
     def kept(bank, c0, c1, tok):
         return V([tok], "ts", T.kept[:, c0:c1], bank[:, 0:c1 - c0], 0.5, None, A.is_gt)
@@ -347,79 +325,58 @@ def rank_program(g, core, T, topo):
         return [(T.b4[:, 0:16], moved(E, s), T.kept[:, 16 * s:16 * s + 16], first and s == s0, last and s == s1 - 1)
                 for s in range(s0, s1)]
 
-    t_k1 = MM(g1 + [v_jl[1]], tlist(T.b1, T.R2x, 0, 128))
-    t_by = MM([r_k, v_jl[3], m_id], back(T.b3, 0, NY, T.kYl))
-    t_k2 = MM(g3 + [v_jl[2]], tlist(T.b2, T.R2x, 128, 160))
-    V([], "ms", T.ones[:], 1.0)
-    v_cc = V([v_pm], "ts", T.ccol[:], T.pm[:], 16.0, None, A.mult)
+    MM([r_f, m_id], plus(T.b7, T.kfl[:, 0:128], False) + plus(T.b5, T.kfl[:, 128:256], False), False)
+    t_k1 = MM(g1 + g2 + [v_jl[1]], tlist(T.b1, T.R2x, 0, 128))
+    v_padc = V([], "ts", T.padc[:], T.pm[:], 0.5, -1.0, A.is_lt, A.mult)
+    v_cc = V([], "ts", T.ccol[:], T.pm[:], 16.0, None, A.mult)
     v_cst = V([v_cc, c_ci], "ts", T.cst[:], T.ci[:], T.ccol[:], None, A.add)
-    v_mc = V([v_mcol, c_mc], "ts", T.mcs[:], T.mc0[:], T.mcol[:], None, A.add)
-    v_k1 = V([t_k1], "cp", T.kX1[:], T.b1[:, 0:128])
+    t_by = MM([r_k, v_jl[3], m_id], back(T.b3, 0, NY, T.kYl))
+    t_y0 = MM([], plus(T.b7, T.kYl[:], True))
+    a_k1 = ACT([t_k1], T.kX1[:], T.b1[:, 0:128], F.Copy)
+    c_mk = ACT([], T.mk[:, 0:1024], T.V2[:, 0:1024], F.Copy, None, 0.0)
     v_cy = kept(T.b3, 0, NY, t_by)
-    t_b1 = MM([v_k1, a_ky], back(T.b0, 96, 224, T.kX1))
-    MM([v_cy, m_e], zsum(0, 4, True, False), False)
-    v_k2 = V([t_k2], "cp", T.kX2[:], T.b2[0:32, 0:128])
-    v_c1 = kept(T.b0, 96, 224, t_b1)
-    t_b2 = MM([v_k2], back(T.b1, 224, 256, T.kX2))
-    v_c2 = kept(T.b1, 224, 256, t_b2)
-    v_e16 = V([m_e], "cp", T.E16[:], T.BO[:, 0:144])
-    V([m_id], "cp", T.I16[:], ID)
-    v_i4k = V([], "ts", T.I4k[:], ID, 4096.0, None, A.mult)
-    MM([], zsum(4, 6, False, False), False)
-    MM([v_c1], zsum(6, 14, False, False), False)
-    t_z = MM([v_c2], zsum(14, 16, False, True))
-    v_zc = V([t_z, v_pb2, v_zx], "scan", T.zx[:, 1:17], T.ones[:, 0:16], T.b4[:, 0:16], 0.0, A.mult, A.add)
-    t_off = MM([v_zc, m_ls], [(T.b5[:, 0:1], LS, T.zx[:, 16:17], True, True)])
+    t_b1 = MM([a_k1], back(T.b0, 128, 256, T.kX1))
+    MM([v_cy, m_e], zsum(0, 8, True, False), False)
+    v_c1 = kept(T.b0, 128, 256, t_b1)
+    v_e4 = V([m_e], "ts", T.E4[:], T.BO[:, 0:144], 256.0, None, A.mult)
+    t_z = MM([v_c1, v_jl[2]], zsum(8, 16, False, True))
+    v_zc = V([t_z, v_zx, v_cst, p_ones], "scan", T.zx[:, 1:17], T.ones[:, 0:16], T.b4[:, 0:16], 0.0, A.mult, A.add)
+    t_y1 = MM([], plus(T.b5, T.kX1[:], True))
+    ACT([t_y0], T.YW[:, 0:128], T.b7[:, 0:128], F.Identity, -3.0)
+    a_yw = ACT([t_y1], T.YW[:, 128:256], T.b5[:, 0:128], F.Identity, -3.0)
+    DMA("s", "dwin", [a_yw], T.WB[1::16, 0:4096], T.YW[:])
+    t_off = MM([v_zc, m_ls], [(T.b1[:, 128:129], LS, T.zx[:, 16:17], True, True)])
     v_e0 = V([t_z], "ts", T.e0[:], T.b4[:, 0:16], 0.0, None, A.is_equal)
     v_e1 = V([v_e0, v_cst], "tt", T.e1[:], T.e0[:], T.cst[:], A.mult)
     v_p1 = V([v_e1, v_zc], "tt", T.p1[:], T.e1[:], T.zx[:, 0:16], A.add)
-    v_zl = V([v_p1, t_off], "ts", T.zl[:], T.p1[:], T.b5[:, 0:1], None, A.add)
+    v_zl = V([v_p1, t_off], "ts", T.zl[:], T.p1[:], T.b1[:, 128:129], None, A.add)
     MM([m_sg], [(T.b3[:, 0:256], SG, T.kept[:], True, True)], False)
     t_n1 = MM([m_nl], [(T.b3[:, 256:512], T.NL[:], T.kept[:], True, True)])
-    MM([], into7(96, 224, T.kX1) + into7(0, NY, T.kYl) + into7(224, 256, T.kX2), False)
-    MM([r_f], into7(0, 128, T.kfl[:, 0:128]) + into7(128, 256, T.kfl[:, 128:256]), False)
-    t_y7 = MM([v_pb2], [(T.b7[:, 0:256], ID, T.parb[:], False, True)])
-    a_yw = ACT([t_y7], T.YW[:], T.b7[:, 0:256], F.Identity, -3.0)
-    v_mks = V([v_zl, c_mk, c_d3], "cp", T.mk[:].indirect(T.zl[:]), T.d3[:])
-    v_blk = V([v_mks], "scan", T.blk[:], T.mk[:, 0:1024], T.mk[:, 0:1024], 0.0, A.max, A.max)
-    t_bl = MM([v_blk, m_b0, v_zl], rewrap(T.b5[:, 64:128], B0, T.blk, 0, 64))
-    v_cum = V([t_n1], "scan", T.cum[:], T.ones[:], T.b3[:, 0:256], -1.5, A.mult, A.add)
-    v_kw = V([v_cum], "tt", T.KW[:], T.b3[:, 256:512], T.cum[:], A.add)
-    v_f = V([v_mc, v_cum], "ts", T.F4[:], T.mcs[:], T.cum[:, 255:256], 4096.0, A.is_le, A.mult)
-    v_bl = V([t_bl], "cp", T.bl[:], T.b5[:, 64:128])
-
-    def osum(dst, src, xs, first, last):
-        return [(dst, T.E16[:, 15 - x:143 - x], src[:, 64 * x:64 * x + 64], first and x == xs[0], last and x == xs[-1])
-                for x in xs]
-
-    PX, PY = T.b4[:, 64:128], T.b6[:, 256:320]
-    bl = [T.bl[:, 0:32], T.bl[:, 32:64]]
-    hs = [(0, 512), (512, 1024)]
-    a_gy = [ACT([a_yw, v_bl], T.gy[:, m0:m1], T.YW[:].indirect(T.bl[:, m0 // 16:m1 // 16]), F.Copy)
-            for m0, m1 in ((0, 512), (512, 640))]
-    v_hit = [V([v_kw, v_bl, c_mi], "tt", T.hit[:, m0:m1], T.KW[:].indirect(bl[h]), T.mi[:, m0:m1], A.is_equal)
-             for h, (m0, m1) in enumerate(hs)]
-    v_hx = [V([v_hit[h], v_xw], "tt", T.hx[:, m0:m1], T.XW[:].indirect(bl[h]), T.hit[:, m0:m1], A.mult)
-            for h, (m0, m1) in enumerate(hs)]
-    v_hy = [V([v_hit[1], a_yw], "tt", T.hy[:, n:n + 192], T.YW[:].indirect(T.bl[:, n // 16:n // 16 + 12]), T.hit[:, n:n + 192],
-              A.mult) for n in (640, 832)]
-    MM([a_gy[0], v_i4k], [(T.b0[:], T.I16[:], T.gy[:, 0:512], True, False)], False)
-    t_m = MM([v_hit[0]], [(T.b0[:], T.I4k[:], T.hit[:, 0:512], False, True)])
-    MM([a_gy[1]], [(T.b1[:, 0:128], T.I16[:], T.gy[:, 512:640], True, False)], False)
-    t_m2 = MM([v_hit[1]], [(T.b1[:, 0:128], T.I4k[:], T.hit[:, 512:640], False, True)])
-    a_hy = ACT([t_m], T.hy[:, 0:512], T.b0[:], F.Relu, -4096.0)
-    a_hy2 = ACT([t_m2], T.hy[:, 512:640], T.b1[:, 0:128], F.Relu, -4096.0)
-    MM([v_hx[0], v_e16, v_zc, v_e1], osum(PX, T.hx, range(0, 8), True, False), False)
-    MM([a_hy, a_kf], osum(PY, T.hy, range(0, 8), True, False), False)
-    MM([a_hy2], osum(PY, T.hy, range(8, 10), False, False), False)
-    t_x = MM([v_hx[1]], osum(PX, T.hx, range(8, 16), False, True))
-    MM([v_hy[0]], osum(PY, T.hy, range(10, 13), False, False), False)
-    t_y = MM([v_hy[1]], osum(PY, T.hy, range(13, 16), False, True))
-    v_ox = V([v_f, t_x], "tt", T.ox[:], PX, T.F4[:], A.add)
-    v_pa = V([t_y], "ts", T.pa[:], PY, 1023.5, -1.0, A.is_ge, A.add)
-    v_pm2 = V([], "ts", T.pc[:], PY, 1023.5, -1024.0, A.is_ge, A.mult)
-    v_ok = V([v_pa, v_ox], "tt", T.ok[:], T.ox[:], T.pa[:], A.add)
-    DMA("s", "dout", [v_ok], T.yk[:], T.ok[:])
-    v_os = V([v_pm2], "tt", T.osum[:], PY, T.pc[:], A.add)
-    DMA("a", "dout", [v_os], T.ys[:], T.osum[:])
+    v_pad = ACT([v_padc, c_mk], T.WB[:, 4096:4352], T.mk[:, 0:256], F.Identity, T.padc[:])
+    v_mks = V([v_zl, c_mk, v_pad, c_d3], "cp", T.mk[:].indirect(T.zl[:]), T.d3[:])
+    v_b0 = V([v_mks], "scan", T.blk[:, 0:512], T.mk[:, 0:512], T.mk[:, 0:512], 0.0, A.max, A.max)
+    v_b1 = V([v_b0], "scan", T.blk[:, 512:1024], T.mk[:, 512:1024], T.mk[:, 512:1024], T.blk[:, 511:512], A.max, A.max)
+    t_bl = [MM([v_b, m_b0], rewrap(b[:, 0:32], B0, T.blk, 32 * h, 32 * h + 32))
+            for h, (v_b, b) in enumerate(((v_b0, T.b0), (v_b1, T.b1)))]
+    v_cum = V([t_n1], "scan", T.cum[:], T.ones[:], T.b3[:, 0:256], 0.0, A.mult, A.add)
+    v_kw = V([v_cum], "tt", T.KW[:], T.cum[:], T.b3[:, 256:512], A.subtract)
+    a_kv = ACT([v_kw], T.KV[:], T.KW[:], F.Identity, -512.0)
+    v_bl, v_hit = [], []
+    for h, (b, kw, tok) in enumerate(((T.b0, T.KW, v_kw), (T.b1, T.KV, a_kv))):
+        lst = T.bl[:, 32 * h:32 * h + 32]
+        v_bl.append(V([t_bl[h]], "cp", lst, b[:, 0:32]))
+        v_hit.append(V([tok, v_bl[h], c_mi], "tt", T.hit[:, 512 * h:512 * h + 512], kw[:].indirect(lst), T.mi[:], A.is_le))
+    t_h = []
+    for h, (b, o) in enumerate(((T.b0, T.b2), (T.b1, T.b6))):
+        a_bc = ACT([v_bl[h]], T.blc[:, 32 * h:32 * h + 32], b[:, 0:32], F.Copy)
+        MM([a_bc], [(o[:, 0:32], ID, T.blc[:, 32 * h:32 * h + 32], True, False)], False)
+        t_h.append(MM([v_hit[h], v_e4], rewrap(o[:, 0:32], E256, T.hit, 32 * h, 32 * h + 32, first=False)))
+    v_of = [V([t_h[h]], "cp", T.off[:, 32 * h:32 * h + 32], o[:, 0:32]) for h, o in enumerate((T.b2, T.b6))]
+    win = T.WB[:, 0:4352]
+    rows = [v_pad, ("dwin", cnt["dwin"])]
+    ACT([v_of[0]] + rows, T.res[:, 0:512], win.indirect(T.off[:, 0:32]), F.Copy)
+    v_r = V([v_of[1]] + rows, "cp", T.res[:, 512:768], win.indirect(T.off[:, 32:48]))
+    a_r = ACT([v_of[1]], T.res[:, 768:1024], win.indirect(T.off[:, 48:64]), F.Copy)
+    DMA("s", "dout", [a_r, v_r], T.yk[:], T.res[0::16, :])
+    DMA("a", "dout", [a_r, v_r], T.ys[:], T.res[1::16, :])
     need("p", [(s, cnt[s]) for s in sorted(cnt)])

from concourse.mybir import AluOpType as A, ActivationFunctionType as F

SCRATCH = {
    "owi": ("sbuf", [128, 256], "int32"),
    "pti": ("sbuf", [128, 256], "int32"),
    "nxi": ("sbuf", [128, 256], "int32"),
    "nls": ("sbuf", [128, 256], "uint16"),
    "nl": ("sbuf", [128, 256], "uint16"),
    "pb": ("sbuf", [128, 256], "bfloat16"),
    "pfB": ("sbuf", [128, 128], "float32"),
    "ltA": ("sbuf", [128, 128], "bfloat16"),
    "htA": ("sbuf", [128, 128], "bfloat16"),
    "ltB": ("sbuf", [128, 128], "float32"),
    "htB": ("sbuf", [128, 128], "float32"),
    "ol": ("sbuf", [128, 256], "uint16"),
    "jl": ("sbuf", [128, 256], "uint16"),
    "jy": ("sbuf", [128, 128], "uint16"),
    "jx": ("sbuf", [128, 128], "uint16"),
    "DA": ("sbuf", [128, 2048], "bfloat16"),
    "DB": ("sbuf", [128, 2048], "float32"),
    "WA": ("sbuf", [128, 8192], "bfloat16"),
    "WB": ("sbuf", [128, 8192], "float32"),
    "bg": ("sbuf", [128, 4096], "bfloat16"),
    "R": ("sbuf", [128, 4112], "bfloat16"),
    "V2": ("sbuf", [128, 4112], "bfloat16"),
    "R2y": ("sbuf", [128, 2048], "bfloat16"),
    "R2x": ("sbuf", [128, 2048], "bfloat16"),
    "prow": ("sbuf", [8, 4096], "bfloat16"),
    "pid": ("sbuf", [128, 1], "int32"),
    "pm": ("sbuf", [128, 1], "int32"),
    "hA": ("sbuf", [128, 1], "float32"),
    "hB": ("sbuf", [128, 1], "float32"),
    "ccol": ("sbuf", [128, 1], "float32"),
    "padc": ("sbuf", [128, 1], "float32"),
    "ci": ("sbuf", [128, 16], "float32"),
    "cst": ("sbuf", [128, 16], "float32"),
    "BZ": ("sbuf", [128, 704], "bfloat16"),
    "BO": ("sbuf", [128, 400], "bfloat16"),
    "NL": ("sbuf", [128, 128], "bfloat16"),
    "E4": ("sbuf", [128, 144], "bfloat16"),
    "ones": ("sbuf", [128, 256], "float32"),
    "d3": ("sbuf", [128, 256], "bfloat16"),
    "mi": ("sbuf", [128, 512], "float32"),
    "mk": ("sbuf", [128, 2320], "bfloat16"),
    "blk": ("sbuf", [128, 1024], "bfloat16"),
    "bl": ("sbuf", [128, 64], "uint16"),
    "blc": ("sbuf", [128, 64], "bfloat16"),
    "off": ("sbuf", [128, 64], "uint16"),
    "kYs": ("sbuf", [128, 128], "bfloat16"),
    "kYl": ("sbuf", [128, 128], "bfloat16"),
    "kX1": ("sbuf", [128, 128], "bfloat16"),
    "kfs": ("sbuf", [128, 256], "bfloat16"),
    "kfl": ("sbuf", [128, 256], "bfloat16"),
    "kept": ("sbuf", [128, 256], "bfloat16"),
    "zx": ("sbuf", [128, 32], "bfloat16"),
    "e0": ("sbuf", [128, 16], "float32"),
    "e1": ("sbuf", [128, 16], "float32"),
    "p1": ("sbuf", [128, 16], "float32"),
    "zl": ("sbuf", [128, 16], "uint16"),
    "cum": ("sbuf", [128, 256], "float32"),
    "KW": ("sbuf", [128, 256], "float32"),
    "KV": ("sbuf", [128, 256], "float32"),
    "YW": ("sbuf", [128, 256], "float32"),
    "owf": ("sbuf", [128, 256], "float32"),
    "hit": ("sbuf", [128, 1024], "bfloat16"),
    "res": ("sbuf", [128, 1024], "float32"),
}
for _k in range(8):
    SCRATCH["b%d" % _k] = ("psum", [128, 512], "float32")
SEMAPHORES = ["v", "a", "t", "p", "down", "dptb", "dpts", "dnxt", "dda", "ddb", "dprow", "dwin", "dout",
              "rn", "rv", "ry0", "ry1", "rx0", "rx1", "rk", "rf", "sent"]

SUBS = [(0, 16), (16, 32)] + [(k, k + 32) for k in range(32, 224, 32)] + [(224, 240), (240, 256)]
SENDS = [(0, 32), (32, 96), (96, 160), (160, 224), (224, 256)]
NY = 128


def rank_program(g, core, T, topo):
    rank = T.rank_of(core)
    if rank is None:
        return
    prv, nxc, opp = (T.cores[(rank + k) % 4] for k in (3, 1, 2))
    queues = {"v": g.vector, "a": g.scalar, "t": g.tensor, "p": g, "s": g.sync}
    cnt = {}
    seen = {}

    def need(q, toks):
        best = {}
        for s, n in toks:
            best[s] = max(best.get(s, 0), n)
        for s in sorted(best):
            if seen.get((q, s), 0) < best[s]:
                queues[q].wait_ge(T.sem[s], best[s])
                seen[(q, s)] = best[s]

    def done(s, ins, n):
        cnt[s] = cnt.get(s, 0) + n
        ins.then_inc(T.sem[s], n)
        return (s, cnt[s])

    def V(toks, name, *args):
        need("v", toks)
        q = g.vector
        if name == "ts":
            out, in0, s1, s2, op0 = args[:5]
            ins = q.tensor_scalar(out, in0, s1, s2, op0, args[5]) if len(args) > 5 else q.tensor_scalar(out, in0, s1, s2, op0)
        elif name == "tt":
            ins = q.tensor_tensor(*args)
        elif name == "cp":
            ins = q.tensor_copy(*args)
        elif name == "ms":
            ins = q.memset(*args)
        else:
            ins = q.tensor_tensor_scan(*args)
        return done("v", ins, 1)

    def ACT(toks, out, in_, func, bias=None, scale=None):
        need("a", toks)
        if scale is not None:
            ins = g.scalar.activation(out, in_, func, scale=scale)
        elif bias is not None:
            ins = g.scalar.activation(out, in_, func, bias=bias)
        else:
            ins = g.scalar.activation(out, in_, func)
        return done("a", ins, 1)

    def IOTA(toks, out, pattern, base, cm, small=True):
        need("p", toks)
        ins = g.iota(out, pattern, base, cm, allow_small_or_imprecise_dtypes=True) if small else g.iota(out, pattern, base, cm)
        return done("p", ins, 1)

    def SEL(toks, buf, pattern, cmp, fill, base, cm):
        need("p", toks)
        return done("p", g.affine_select(buf, buf, pattern, cmp, fill, base, cm), 1)

    def SELO(toks, out, src, pattern, cmp, base, cm):
        need("p", toks)
        return done("p", g.affine_select(out, src, pattern, cmp, 0.0, base, cm), 1)

    def DMA(q, s, toks, out, in_):
        need(q, toks)
        return done(s, queues[q].dma_start(out, in_), 16)

    def MM(toks, jobs, tok=True):
        need("t", toks)
        ins = None
        for out, lhs, rhs, st, sp in jobs:
            ins = g.tensor.matmul(out, lhs, rhs, st, sp)
        return done("t", ins, 1) if tok else None

    def SEND(toks, to, dst, src, sem):
        need("p", toks)
        rid, pid, _se = topo.addr(to)
        g.remote_dma(out_ap=dst, in_ap=src, remote_sem=T.sem[sem], local_sem=T.sem.sent, pid=pid, routing_id=rid,
                     dma_engine_mask=topo.mask(core, to))
        n = len(topo.engines(core, to))
        cnt["sent"] = cnt.get("sent", 0) + n
        cnt[sem] = cnt.get(sem, 0) + n
        return (sem, cnt[sem])

    def moved(mat, t, K=128):
        buf, c = mat
        return buf[0:K, c + 15 - t:c + 143 - t]

    def rewrap(out, mat, src, c0, c1, K=128, close=True, first=True):
        return [(out, moved(mat, t, K), src[0:K, 16 * c0 + t:16 * c1:16], first and t == 0, close and t == 15)
                for t in range(16)]

    def el(buf, c0, c1):
        return buf[:, 16 * c0:16 * c1]

    l_own = DMA("s", "down", [], T.owi[:], T.own[:])
    l_ptb = DMA("a", "dptb", [], T.pti[:, 128:256], T.pts[:, 2048:4096])
    l_pts = DMA("a", "dpts", [], T.pti[:, 0:128], T.pts[:, 0:2048])
    l_nxt = DMA("s", "dnxt", [], T.nxi[:], T.nxt[:])

    c_pid = IOTA([], T.pid[:], [[1, 1]], 0, 1, False)
    c_lta = IOTA([], T.ltA[:], [[-16, 128]], 2048, 0)
    c_ltb = IOTA([], T.ltB[:], [[-16, 128]], 2048, 0)
    z0 = V([], "ms", T.WB[:, 0:128], 0.0)
    v_da = V([], "ms", T.DA[:], 0.0)
    z1 = V([], "ms", T.WB[:, 256:1024], 0.0)
    v_db = V([], "ms", T.DB[:, 0:640], 0.0)
    v_pm = V([c_pid], "ts", T.pm[:], T.pid[:], 15, None, A.bitwise_and)
    v_ha = V([v_pm], "ts", T.hA[:], T.pm[:], -16.0, 496.0, A.mult, A.add)
    v_hb = V([v_pm], "ts", T.hB[:], T.pm[:], -16.0, 240.0, A.mult, A.add)
    a1 = ACT([z0], T.WB[:, 128:256], T.WB[:, 0:128], F.Silu)
    ACT([a1, z1], T.DB[:, 640:1664], T.WB[:, 0:1024], F.Silu)
    a2 = ACT([], T.DB[:, 1664:2048], T.WB[:, 0:384], F.Silu)
    a_htb = ACT([v_hb], T.htB[:], T.WB[:, 0:128], F.Identity, T.hB[:])
    a_hta = ACT([v_ha], T.htA[:], T.WB[:, 0:128], F.Identity, T.hA[:])
    a3 = ACT([], T.WB[:, 1024:2048], T.WB[:, 0:1024], F.Silu)
    ACT([a3], T.WB[:, 2048:4096], T.WB[:, 0:2048], F.Silu)
    a5 = ACT([a3], T.WB[:, 4096:5248], T.WB[:, 0:1152], F.Silu)
    v_pfb = V([l_ptb], "ts", T.pfB[:], T.pti[:, 128:256], 16.0, 16.0, A.mult, A.add)
    V([], "ms", T.WA[:, 0:2048], 0.0)
    v_ol = V([l_own], "cp", T.ol[:], T.owi[:])
    v_pb = V([l_pts], "ts", T.pb[:], T.pti[:], 16.0, 16.0, A.mult, A.add)
    V([], "ms", T.WA[:, 2048:5120], 0.0)
    v_nls = V([l_nxt], "cp", T.nls[:], T.nxi[:])
    v_wa = V([], "ms", T.WA[:, 5120:8192], 0.0)
    DMA("s", "dda", [v_da, c_lta], T.DA[1::16, :], T.ltA[:])
    DMA("s", "ddb", [v_db, a2, c_ltb], T.DB[1::16, :], T.ltB[:])
    DMA("s", "ddb", [v_pfb], T.DB[2::16, :], T.pfB[:])
    d_b = DMA("s", "ddb", [a_htb], T.DB[0::16, :], T.htB[:])
    DMA("s", "dda", [a_hta], T.DA[0::16, :], T.htA[:])
    d_a = DMA("s", "dda", [v_pb], T.DA[2::16, :], T.pb[:, 0:128])
    DMA("s", "dprow", [], T.prow[:, 0:2048], T.pb[:, 0:128])
    d_prow = DMA("s", "dprow", [], T.prow[:, 2048:4096], T.pb[:, 128:256])

    IOTA([], T.WB[:, 5248:6720], [[0, 1472]], 0, 0)
    p_z2 = IOTA([], T.WB[:, 6720:8192], [[0, 1472]], 0, 0)
    r_n = SEND([v_nls], nxc, T.nl[:], T.nls[:], "rn")
    p_z = IOTA([], T.BZ[:], [[0, 704]], 0, 0)

    s_b = ACT([a5, p_z2, v_ol, d_b], T.WB[:].indirect(T.ol[:, 128:256]), T.DB[:], F.Silu)
    s_a = V([v_wa, v_ol, d_a], "cp", T.WA[:].indirect(T.ol[:, 0:128]), T.DA[:])

    BI, B2, B0, B8 = ((T.BZ, 144 * k) for k in range(4))
    ID = T.BZ[:, 576:704]
    E = (T.BO, 0)
    E256 = (T.E4, 0)
    LS = T.BO[:, 144:272]
    SG = T.BO[:, 272:400]

    def rowsel(mat, fills):
        buf = mat[0][:, mat[1]:mat[1] + 144]
        tok = p_z
        for k, w in fills:
            tok = SEL([tok], buf, [[-16, 9], [0, 16]], A.not_equal, w, -k, 1)
        return SEL([tok], buf, [[0, 9], [1, 16]], A.is_equal, 0.0, -15, 0)

    m_bi = rowsel(BI, [(0, 8.0), (1, 0.0625)])
    m_b8 = SEL([p_z], T.BZ[:, 432:576], [[-1, 144]], A.not_equal, 0.0625, 15, 16)
    m_b2 = rowsel(B2, [(2, 0.0625)])
    IOTA([], T.R[:, 4096:4112], [[0, 16]], 0, 0)
    IOTA([], T.V2[:, 4096:4112], [[0, 16]], 0, 0)
    v_zx = IOTA([], T.zx[:], [[0, 32]], 0, 0)
    m_id = SEL([p_z], ID, [[-1, 128]], A.not_equal, 1.0, 0, 1)
    IOTA([], T.BO[:, 128:144], [[0, 16]], 0, 0)
    p_one = IOTA([], SG, [[0, 128]], 1, 0)

    MM([m_b8, d_prow], rewrap(T.b7[:, 0:128], B8, T.prow, 0, 128, 8, False)
       + rewrap(T.b5[:, 0:128], B8, T.prow, 128, 256, 8, False), False)

    def tlist(out, src, c0, c1):
        return [(out[0:c1 - c0, t:128:16], src[:, 16 * c0 + t:16 * c1:16], T.BZ[:, 159:287:16], True, True)
                for t in range(16)]

    g_a = [ACT([s_b, r_n], el(T.bg, c0, c1), T.WB[:].indirect(T.nl[:, c0:c1]), F.Copy) for c0, c1 in SUBS]
    upto = {}
    t_code = [None] * 4
    v_jl = [None] * 4

    def jl(q):
        v_jl[q] = V([t_code[q]], "ts", T.jl[:, 64 * q:64 * q + 64], T["b%d" % q][:, 0:64], -1.0, 4096.0, A.mult, A.add)

    r_y, r_x = [], []
    for k, (c0, c1) in enumerate(SUBS):
        upto[c1] = V([s_a, g_a[k], r_n], "tt", el(T.R, c0, c1), T.WA[:].indirect(T.nl[:, c0:c1]), el(T.bg, c0, c1), A.add)
        for s0, s1 in SENDS:
            if s1 == c1:
                r_v = SEND([upto[c1]], opp, el(T.V2, s0, s1), el(T.R, s0, s1), "rv")
        if c1 % 64 == 0:
            q = c1 // 64 - 1
            t_code[q] = MM([upto[c1], m_bi], rewrap(T["b%d" % q][:, 0:64], BI, T.R, 64 * q, 64 * q + 64))
            if q == 1:
                MM([m_b2], tlist(T.b6[:, 0:128], T.R, 0, 128), False)
        if c1 == 32:
            m = SEL([p_one], SG, [[-16, 8], [0, 16]], A.is_ge, 0.0, 0, 1)
        if c1 == 96:
            m_sg = SEL([m], SG, [[16, 8], [0, 16]], A.is_ge, 0.0, 15, -1)
        if c1 == 128:
            jl(0)
            r_y.append(SEND([v_jl[0]], nxc, T.jy[:, 0:64], T.jl[:, 0:64], "ry0"))
        if c1 == 160:
            m_e = SELO([m_sg], T.BO[:, 0:128], SG, [[0, 8], [1, 16]], A.is_equal, -15, 0)
        if c1 == 192:
            jl(1)
            r_y.append(SEND([v_jl[1]], nxc, T.jy[:, 64:NY], T.jl[:, 64:NY], "ry1"))
        if c1 == 240:
            jl(2)
            r_x.append(SEND([v_jl[2]], prv, T.jx[:, 0:192 - NY], T.jl[:, NY:192], "rx0"))

    gy2 = []
    for r, (c0, cm, c1) in zip(r_y, ((0, 32, 64), (64, 96, NY))):
        gy2.append(V([upto[256], r, v_zx], "cp", el(T.R2y, c0, cm), T.R[:].indirect(T.jy[:, c0:cm])))
        gy2.append(ACT([upto[256], r, v_zx], el(T.R2y, cm, c1), T.R[:].indirect(T.jy[:, cm:c1]), F.Copy))
        if c0 == 0:
            v_owf = V([l_own], "cp", T.owf[:], T.owi[:])
            jl(3)
            r_x.append(SEND([v_jl[3]], prv, T.jx[:, 192 - NY:256 - NY], T.jl[:, 192:256], "rx1"))
    c_ci = IOTA([], T.ci[:], [[1, 16]], 1025, 0)
    t_kf = MM([m_b2], tlist(T.b6[:, 128:256], T.R, 128, 256))
    a_kf = ACT([t_kf], T.kfs[:], T.b6[:, 0:256], F.Copy)
    r_f = SEND([a_kf], prv, T.kfl[:], T.kfs[:], "rf")
    t_ky = MM(gy2 + [v_jl[0]], tlist(T.b0, T.R2y, 0, NY))
    a_ky = ACT([t_ky], T.kYs[:], T.b0[:, 0:128], F.Copy)
    r_k = SEND([a_ky], opp, T.kYl[:], T.kYs[:], "rk")
    p_ones = IOTA([], T.ones[:], [[0, 256]], 1, 0)
    c_d3 = IOTA([], T.d3[:], [[16, 16], [256, 16]], 0, 0)
    m_ls = SELO([m_sg], LS, SG, [[1, 128]], A.is_gt, 0, -1)
    m_nl = SELO([m_sg], T.NL[:], SG, [[-1, 128]], A.is_gt, 0, 1)
    m_b0 = rowsel(B0, [(0, 0.0625)])
    c_mi = IOTA([], T.mi[:], [[1, 512]], 0, 0)

    def gx(c0, c1):
        return el(T.R2x, c0 - NY, c1 - NY), T.V2[:].indirect(T.jx[:, c0 - NY:c1 - NY])

    g1 = [V([r_v, r_x[0], v_zx], "cp", *gx(128, 164)), ACT([r_v, r_x[0], v_zx], *gx(164, 192), F.Copy)]
    g2 = [V([r_x[1]], "cp", *gx(192, 224)), ACT([r_x[1]], *gx(224, 256), F.Copy)]
    DMA("s", "dwin", [v_owf, g_a[-1], g2[1]], T.WB[0::16, 0:4096], T.owf[:])

    def back(bank, c0, c1, kt):
        n = c1 - c0
        return [(bank[:, 0:n], kt[0:n, :], ID[0:n, 0:n], True, True)]

    def plus(bank, kt, last):
        return [(bank[:, 0:128], kt, ID, False, last)]

    def kept(bank, c0, c1, tok):
        return V([tok], "ts", T.kept[:, c0:c1], bank[:, 0:c1 - c0], 0.5, None, A.is_gt)

    def zsum(s0, s1, first, last):
        return [(T.b4[:, 0:16], moved(E, s), T.kept[:, 16 * s:16 * s + 16], first and s == s0, last and s == s1 - 1)
                for s in range(s0, s1)]

    MM([r_f, m_id], plus(T.b7, T.kfl[:, 0:128], False) + plus(T.b5, T.kfl[:, 128:256], False), False)
    t_k1 = MM(g1 + g2 + [v_jl[1]], tlist(T.b1, T.R2x, 0, 128))
    v_padc = V([], "ts", T.padc[:], T.pm[:], 0.5, -1.0, A.is_lt, A.mult)
    v_cc = V([], "ts", T.ccol[:], T.pm[:], 16.0, None, A.mult)
    v_cst = V([v_cc, c_ci], "ts", T.cst[:], T.ci[:], T.ccol[:], None, A.add)
    t_by = MM([r_k, v_jl[3], m_id], back(T.b3, 0, NY, T.kYl))
    t_y0 = MM([], plus(T.b7, T.kYl[:], True))
    a_k1 = ACT([t_k1], T.kX1[:], T.b1[:, 0:128], F.Copy)
    c_mk = ACT([], T.mk[:, 0:1024], T.V2[:, 0:1024], F.Copy, None, 0.0)
    v_cy = kept(T.b3, 0, NY, t_by)
    t_b1 = MM([a_k1], back(T.b0, 128, 256, T.kX1))
    MM([v_cy, m_e], zsum(0, 8, True, False), False)
    v_c1 = kept(T.b0, 128, 256, t_b1)
    v_e4 = V([m_e], "ts", T.E4[:], T.BO[:, 0:144], 256.0, None, A.mult)
    t_z = MM([v_c1, v_jl[2]], zsum(8, 16, False, True))
    v_zc = V([t_z, v_zx, v_cst, p_ones], "scan", T.zx[:, 1:17], T.ones[:, 0:16], T.b4[:, 0:16], 0.0, A.mult, A.add)
    t_y1 = MM([], plus(T.b5, T.kX1[:], True))
    ACT([t_y0], T.YW[:, 0:128], T.b7[:, 0:128], F.Identity, -3.0)
    a_yw = ACT([t_y1], T.YW[:, 128:256], T.b5[:, 0:128], F.Identity, -3.0)
    DMA("s", "dwin", [a_yw], T.WB[1::16, 0:4096], T.YW[:])
    t_off = MM([v_zc, m_ls], [(T.b1[:, 128:129], LS, T.zx[:, 16:17], True, True)])
    v_e0 = V([t_z], "ts", T.e0[:], T.b4[:, 0:16], 0.0, None, A.is_equal)
    v_e1 = V([v_e0, v_cst], "tt", T.e1[:], T.e0[:], T.cst[:], A.mult)
    v_p1 = V([v_e1, v_zc], "tt", T.p1[:], T.e1[:], T.zx[:, 0:16], A.add)
    v_zl = V([v_p1, t_off], "ts", T.zl[:], T.p1[:], T.b1[:, 128:129], None, A.add)
    MM([m_sg], [(T.b3[:, 0:256], SG, T.kept[:], True, True)], False)
    t_n1 = MM([m_nl], [(T.b3[:, 256:512], T.NL[:], T.kept[:], True, True)])
    v_pad = ACT([v_padc, c_mk], T.WB[:, 4096:4352], T.mk[:, 0:256], F.Identity, T.padc[:])
    v_mks = V([v_zl, c_mk, v_pad, c_d3], "cp", T.mk[:].indirect(T.zl[:]), T.d3[:])
    v_b0 = V([v_mks], "scan", T.blk[:, 0:512], T.mk[:, 0:512], T.mk[:, 0:512], 0.0, A.max, A.max)
    v_b1 = V([v_b0], "scan", T.blk[:, 512:1024], T.mk[:, 512:1024], T.mk[:, 512:1024], T.blk[:, 511:512], A.max, A.max)
    t_bl = [MM([v_b, m_b0], rewrap(b[:, 0:32], B0, T.blk, 32 * h, 32 * h + 32))
            for h, (v_b, b) in enumerate(((v_b0, T.b0), (v_b1, T.b1)))]
    v_cum = V([t_n1], "scan", T.cum[:], T.ones[:], T.b3[:, 0:256], 0.0, A.mult, A.add)
    v_kw = V([v_cum], "tt", T.KW[:], T.cum[:], T.b3[:, 256:512], A.subtract)
    a_kv = ACT([v_kw], T.KV[:], T.KW[:], F.Identity, -512.0)
    v_bl, v_hit = [], []
    for h, (b, kw, tok) in enumerate(((T.b0, T.KW, v_kw), (T.b1, T.KV, a_kv))):
        lst = T.bl[:, 32 * h:32 * h + 32]
        v_bl.append(V([t_bl[h]], "cp", lst, b[:, 0:32]))
        v_hit.append(V([tok, v_bl[h], c_mi], "tt", T.hit[:, 512 * h:512 * h + 512], kw[:].indirect(lst), T.mi[:], A.is_le))
    t_h = []
    for h, (b, o) in enumerate(((T.b0, T.b2), (T.b1, T.b6))):
        a_bc = ACT([v_bl[h]], T.blc[:, 32 * h:32 * h + 32], b[:, 0:32], F.Copy)
        MM([a_bc], [(o[:, 0:32], ID, T.blc[:, 32 * h:32 * h + 32], True, False)], False)
        t_h.append(MM([v_hit[h], v_e4], rewrap(o[:, 0:32], E256, T.hit, 32 * h, 32 * h + 32, first=False)))
    v_of = [V([t_h[h]], "cp", T.off[:, 32 * h:32 * h + 32], o[:, 0:32]) for h, o in enumerate((T.b2, T.b6))]
    win = T.WB[:, 0:4352]
    rows = [v_pad, ("dwin", cnt["dwin"])]
    ACT([v_of[0]] + rows, T.res[:, 0:512], win.indirect(T.off[:, 0:32]), F.Copy)
    v_r = V([v_of[1]] + rows, "cp", T.res[:, 512:768], win.indirect(T.off[:, 32:48]))
    a_r = ACT([v_of[1]], T.res[:, 768:1024], win.indirect(T.off[:, 48:64]), F.Copy)
    DMA("s", "dout", [a_r, v_r], T.yk[:], T.res[0::16, :])
    DMA("a", "dout", [a_r, v_r], T.ys[:], T.res[1::16, :])
    need("p", [(s, cnt[s]) for s in sorted(cnt)])
